import numpy as np, ml_dtypes
CORES = [3,7,11,15,131,135,139,143]
N = 8
import mx_ref
BF = ml_dtypes.bfloat16
def gentries(a):
    return np.ascontiguousarray(a.reshape(8, 16, -1).transpose(0, 2, 1)).reshape(8, -1)
def gtable(e):
    e = np.asarray(e); return np.ascontiguousarray(e.reshape(8, -1, 16).transpose(0, 2, 1)).reshape(128, -1).astype(np.int32)
def gcols(t, e):
    v = np.concatenate([t.reshape(8, 16, -1, 4), np.zeros((8, 16, 1, 4), BF)], axis=2)
    return np.ascontiguousarray(np.stack([v[g][:, e[g]] for g in range(8)])).reshape(128, -1)
def tile(rs):
    return np.stack(rs, axis=2).reshape(128, -1).astype(BF)
def pick(q, e):
    c = np.concatenate([q[0].reshape(128, -1, 4), np.zeros((128, 1, 4), np.uint8)], axis=1); s = np.concatenate([q[1], np.ones((16, 1), np.uint8)], axis=1)
    return (np.ascontiguousarray(c[:, e].reshape(128, -1)), np.ascontiguousarray(s[:, e]))
def join(*qs):
    return (np.concatenate([q[0] for q in qs], axis=1), np.concatenate([q[1] for q in qs], axis=1))
def put(q, e, v):
    c, s = q[0].reshape(128, -1, 4).copy(), q[1].copy(); c[:, e] = v[0].reshape(128, -1, 4); s[:, e] = v[1]
    return (c.reshape(128, -1), s)
def pk(c, s):
    return (np.ascontiguousarray(c), mx_ref.live(s))
def emit(q):
    return q[0], q[1]
def packed(v, rng):
    q = [mx_ref.quantize(np.ascontiguousarray(v[r])) for r in range(N)]
    return np.stack([a for a, b in q]), np.stack([mx_ref.plane(b, rng) for a, b in q])
def values_of_codes():
    e, c = np.zeros((128, 128, 4), np.float32), np.zeros((128, 2, 4), np.uint8)
    e[np.arange(128), np.arange(128), 0] = 1
    c[:127, :, 0] = np.arange(256).reshape(2, 128).T[:127]
    return mx_ref.matmul(mx_ref.quantize(e.reshape(128, 512).astype(BF)), (c.reshape(128, 8), np.full((16, 2), 127, np.uint8))).T.reshape(-1).astype(np.float64)
CODE_VALUE, SCALE_VALUE = values_of_codes(), 2.0 ** (np.arange(256) - 127.0)
def decode(q):
    return (CODE_VALUE[q[0]].reshape(16, 8, -1, 4) * SCALE_VALUE[q[1]][:, None, :, None] + 0.0).reshape(128, -1).astype(np.float32)
def f(rng, *shape):
    return mx_ref.flush((rng.standard_normal(shape, dtype=np.float32) * np.exp2(rng.integers(-2, 3, shape[:-1] + (1,)))).astype(BF))
def wide(rng, *shape, cols=0):
    v = rng.standard_normal(shape, dtype=np.float32) * np.exp2(rng.integers(-12, 13, shape)).astype(np.float32)
    if cols: v *= np.repeat(np.exp2(rng.integers(-cols, cols + 1, shape[:-2] + (1, shape[-1] // 4))) * (rng.random(shape[:-2] + (1, shape[-1] // 4)) > 0.0625), 4, axis=-1).astype(np.float32)
    return mx_ref.flush(v.astype(BF))
C, H, R = 256, 96, 3
def big(v):
    v = v.astype(np.float32)
    v[np.abs(v) < np.float32(2.0 ** -16)] = 0
    return v.astype(BF)
def numbers_of(rng):
    return {"x": big(f(rng, N, 128, 4 * C)), "u": np.array(f(rng, N, 128, 512)), "v": np.array(f(rng, N, 128, 512))}
def layers(rng, still=[]):
    w = big(f(rng, N, 128, 2048)).reshape(N, 8, 16, 4, 8, 16, 4)
    for i in still: w[:, :, :, :, :, i] = 0
    return w
def weights(rng, w):
    c, s = packed(np.ascontiguousarray(w).reshape(N, 128, 2048), rng)
    return {"wc": c, "ws": s}
def holes(rng):
    return np.sort(np.argsort(rng.random((N, 8, C - 1)), axis=2)[:, :, :H], axis=2)
def throws(rng, a):
    free = np.ones((N, 8, 2 * C), bool)
    free[:, :, C:] = False
    np.put_along_axis(free, a, False, axis=2)
    np.put_along_axis(free, C + np.roll(a, -1, axis=0), True, axis=2)
    e = np.zeros((N, 8, C), np.int64)
    for i in range(C - 1, -1, -1):
        k = (0.5 + rng.random((N, 8, C))) * free[:, :, i:i + C]
        k[:, :, C - 1] = 2.0 * free[:, :, i + C - 1]
        e[:, :, i] = i + np.argmax(k, axis=2)
        np.put_along_axis(free, e[:, :, i:i + 1], False, axis=2)
    return e
def lists(e):
    return np.stack([gtable(e[r]) for r in range(N)])
def meet(rng, e):
    used, out = [False] * C, []
    e = e.tolist()
    for i, k in zip(rng.permutation(C).tolist(), rng.integers(0, 4, C).tolist()):
        j = e[i] + (0, 1, 1 - C, -C)[k]
        if 0 <= j < C and j != i and not used[i] and not used[j]:
            used[i] = used[j] = True
            out += [i, j]
    return np.array(out + [int(i) for i in rng.permutation(C) if not used[i]])
def setup_inputs(rng):
    return {**numbers_of(rng), "p": lists(throws(rng, holes(rng))), **weights(rng, layers(rng))}
def setup_inputs_ties(rng):
    d = numbers_of(rng)
    o = rng.permutation(N)
    x = d["x"].reshape(N, 8, 16, C, 4)
    k = rng.integers(0, 3, (N, 8, C))
    k[o[2]] = 1
    x[:, :, 0] = 0
    x[:, :, 0, :, 0] = k.astype(np.float32).astype(BF)
    u = d["u"].reshape(N, 128, 128, 4)
    u[:, :, ::16] = 0
    for r in range(N):
        for h in range(0, 128, 16): u[r, h, h, 0] = 0.0 if r == o[0] else -1.0 if r == o[1] else 1.0
    return {"x": x.reshape(N, 128, 4 * C), "u": u.reshape(N, 128, 512), "v": d["v"], "p": lists(throws(rng, holes(rng))), **weights(rng, layers(rng, [0]))}
def setup_inputs_near(rng):
    d = numbers_of(rng)
    o = rng.permutation(N) % 4
    low = rng.permutation(8)[:4]
    x = d["x"].astype(np.float32).reshape(N, 8, 16, C, 4)
    u = d["u"].reshape(N, 128, 128, 4)
    x[:, :, 0] = 0
    x[:, :, 8:] = 0
    u[:, :, ::16] = 0
    for r in range(N):
        k = 1.0 if o[r] == 0 else 2.0 ** -30
        if o[r] < 3:
            s = rng.integers(0, 16, (8, C))
            x[r, :, 8] = ((s[:, :, None] >> np.arange(4)) & 1) * np.exp2(np.arange(4) - 23.0)
        else:
            x[r, :, 8, :, 0] = rng.integers(8, 16, (8, C)) * rng.choice([-1.0, 1.0], (8, C)) * 2.0 ** -27
            for g in low: x[r, g, 8:10, :, 0] = rng.integers(8, 15, (2, C)) * 2.0 ** -30
        if o[r] < 2:
            x[r, :, 0, :, 0] = rng.choice([-1.0, 1.0], (8, C))
            x[r, :, 11, :, 0] = 2.0 ** -10
        if o[r] == 2:
            for g in rng.permutation(8)[:4]: x[r, g, 0, rng.integers(C), 0] = 2.0 ** 29
        for h in range(0, 128, 16):
            u[r, h + 8, h] = k
            if o[r] < 2:
                u[r, h, h, 0] = k
                u[r, h + 11, h, 0] = k
            if o[r] == 2: u[r, h, h, 0] = 1.0
            if o[r] == 3 and h // 16 in low: u[r, h + 9, h] = -k
    still = [0, 8, 9, 10, 11, 12, 13, 14, 15]
    w = layers(rng, still)
    w[:, :, still] = 0
    return {"x": x.reshape(N, 128, 4 * C).astype(BF), "u": u.reshape(N, 128, 512), "v": d["v"], "p": lists(throws(rng, holes(rng))), **weights(rng, w)}
def setup_inputs_huge(rng):
    d = numbers_of(rng)
    h, o = rng.permutation(8), rng.permutation(N)
    c = rng.choice([-1.0, 1.0], (N, 1, 1, C, 1))
    c[o == 0] = 1.0
    x = (0.9 + 0.1 * rng.random((N, 8, 16, C, 4))) * 2.0 ** 30
    x[:, h[4:]] *= c
    a = (0.9 + 0.1 * rng.random((N, 8, 16, 8, 4))) * 2.0 ** 30
    for r in range(N):
        if o[r] == 0: a[r] *= -1.0
        elif o[r] % 2 == 1:
            a[r] *= -1.0
            a[r, h[4:]] = 0
        else: a[r, h[:4]] = 0
    u = d["u"].reshape(N, 128, 128, 4)
    u[:, :, ::16] = a.reshape(N, 128, 8, 4).astype(np.float32).astype(BF)
    w = np.zeros((N, 128, 4, 128, 4), np.float32)
    i = np.arange(128)
    for b in range(4): w[:, i, b, i, b] = -1
    return {"x": x.astype(np.float32).reshape(N, 128, 4 * C).astype(BF), "u": u.reshape(N, 128, 512), "v": d["v"], "p": lists(throws(rng, holes(rng))), **weights(rng, w.astype(BF))}
def setup_inputs_edges(rng):
    d = numbers_of(rng)
    h, a = rng.permutation(8), holes(rng)
    a[:, h[:2]] = np.arange(H)
    a[:, h[2:4]] = np.arange(C - 1 - H, C - 1)
    e = throws(rng, a)
    e[:, h[:2]] = np.arange(C) + H
    x = d["x"].reshape(N, 8, 16, C, 4)
    x[:, :, :3] = 0
    for r in range(N):
        for g in range(8):
            n = np.zeros(C, np.int64)
            n[meet(rng, e[r, g])] = np.arange(C - 1, -1, -1)
            for i in range(3): x[r, g, i, :, 0] = ((n >> (6 - 3 * i)) & 7).astype(np.float32).astype(BF)
    k = np.exp2(rng.integers(-2, 3, (N, 8, 1, C, 1)))
    b = (2 * rng.integers(0, 8, (N, 8, 8, C, 4)) + 1) * 2.0 ** -16 * k
    b[:, :, 0, :, 0] = 1.96875 * k[:, :, 0, :, 0]
    b *= rng.choice([-1.0, 1.0], b.shape)
    x[:, :, 8:] = b.astype(np.float32).astype(BF)
    u = d["u"].reshape(N, 128, 128, 4)
    u[:, :, ::16] = 0
    for g in range(0, 128, 16):
        for i in range(3): u[:, g + i, g, 0] = 2.0 ** (6 - 3 * i)
    return {"x": x.reshape(N, 128, 4 * C), "u": u.reshape(N, 128, 512), "v": d["v"], "p": lists(e), **weights(rng, layers(rng, [0, 1, 2, 8, 9, 10, 11, 12, 13, 14, 15]))}
def setup_inputs_spread(rng):
    d = setup_inputs(rng)
    d["x"] = big(wide(rng, N, 128, 4 * C, cols=6))
    return d
def check_inputs(d):
    b = []
    for k in ("x", "u", "v"):
        a = np.abs(d[k].astype(np.float32))
        if not (np.isfinite(a).all() and ((a == 0) | (a >= 2.0 ** -30) & (a <= 2.0 ** 30)).all()): b.append("a value of " + k)
    e = np.stack([gentries(d["p"][r]) for r in range(N)]).astype(np.int64)
    t, s = e - np.arange(C), np.sort(e, axis=2)
    if ((t < 0) | (t >= C)).any(): b.append("p: a landing out of its column's bounds")
    if (s[:, :, 1:] == s[:, :, :-1]).any(): b.append("p: equal landings")
    if (np.count_nonzero(e >= C, axis=2) != H).any(): b.append("p: the number of crossing landings")
    k = np.concatenate([s[:, :, :C - H], np.roll(s[:, :, C - H:], 1, axis=0) - C], axis=2)
    if (np.sort(k, axis=2) != np.arange(C)).any(): b.append("p: crossing landings aren't the next rank's holes")
    none, least, most = [emit(mx_ref.quantize(np.full((128, 16), k, np.float32).astype(BF)))[1][0, 0] for k in (0.0, 2.0 ** -30, 2.0 ** 30)]
    for r in range(N):
        if ((d["wc"][r] == 0x7F) | (d["wc"][r] == 0xFF)).any(): b.append("wc: a code that is no number")
        s = mx_ref.live(d["ws"][r])
        if ((s != none) & ((s < least) | (s > most))).any(): b.append("ws: a scale out of range")
    return b
def reference(x, u, v, p, wc, ws):
    qu = [mx_ref.quantize(u[r]) for r in range(N)]
    lay = [pk(wc[r], ws[r]) for r in range(N)]
    now = [x[r] for r in range(N)]
    land = np.stack([gentries(p[r]) for r in range(N)]).astype(np.int64)
    for t in range(R):
        for r in range(N):
            s = mx_ref.matmul(qu[r], mx_ref.quantize(now[r]))[::16] + np.float32(0.0)
            o = np.argsort(-s, axis=1, kind="stable")
            a, b = o[:, ::2], o[:, 1::2]
            la, lb = np.take_along_axis(land[r], a, axis=1), np.take_along_axis(land[r], b, axis=1)
            ok = (a <= lb) & (lb < a + C) & (b <= la) & (la < b + C)
            np.put_along_axis(land[r], a, np.where(ok, lb, la), axis=1)
            np.put_along_axis(land[r], b, np.where(ok, la, lb), axis=1)
        back, hits = np.argsort(land, axis=2), np.sort(land, axis=2)
        given = [mx_ref.quantize(gcols(now[r], back[r][:, C - H:])) for r in range(N)]
        new = []
        for r in range(N):
            both = np.concatenate([now[r], decode(given[r - 1]).astype(BF)], axis=1)
            e = np.zeros((8, C), np.int64)
            np.put_along_axis(e, hits[r][:, :C - H], back[r][:, :C - H], axis=1)
            np.put_along_axis(e, hits[r - 1][:, C - H:] - C, np.stack([C + np.arange(H)] * 8), axis=1)
            z = ((gcols(both, e).astype(np.float32) + now[r].astype(np.float32)) * np.float32(0.5)).astype(BF)
            q = mx_ref.quantize(z)
            new.append(tile([mx_ref.matmul(pick(lay[r], np.arange(128 * b, 128 * b + 128)), q) * np.float32(0.03125) + z[:, b::4].astype(np.float32) for b in range(4)]))
        now = new
    y, ol = np.zeros((N, 128, C), np.float32), np.zeros((N, 8, C), np.float32)
    oc, osc = np.zeros((N, 128, 4 * C), np.uint8), np.zeros((N, 16, C), np.uint8)
    for r in range(N):
        q = mx_ref.quantize(now[r])
        y[r] = mx_ref.matmul(mx_ref.quantize(v[r]), q)
        ol[r] = land[r]
        oc[r], osc[r] = emit(q)
    return {"y": y, "ol": ol, "oc": oc, "osc": osc}

@@ -1,0 +1,376 @@
+from concourse.mybir import dt, AluOpType, ActivationFunctionType
+
+OP = AluOpType
+AF = ActivationFunctionType
+ROUNDS = 3
+BIG = 1e29
+LIFT = 4096.0
+OFF = 0.46875
+FIELD = sum(1 << b for b in (8, 9, 18, 19, 20))
+PAIR = 254 + 512
+
+CTILES = [("a", 256, ["b", 15, 14, 13]), ("b", 192, [12, 11, 10, 9]), ("c", 128, [8, 7, 6, 5]), ("d", 128, [4, 3, 2, 1])]
+ON_SCALAR = [15, 12]
+
+PACKS = {
+    "rows": (256, "float32", ["irow", "irs", "ex", "yy", "fy", "sx", "so", "vr0", "vr1", "vr2", "lr0", "lr1", "lr2", "lr3", "kwa", "kwb"]),
+    "flist": (16, "float32", ["r16", "q1", "q2", "r1", "ok", "ok1", "y", "zl", "e1", "e2", "own", "neg", "lk", "i1k"]),
+    "ilist": (16, "int32", ["m16", "mm", "ii", "ss", "tt", "c1", "rho", "sig", "tso", "its", "lst1", "lst2", "lst3"]),
+    "iwide": (32, "int32", ["pq", "pm"]),
+    "ulist": (16, "uint16", ["perm", "l16", "sig16", "ts16"]),
+    "cols": (1, "float32", ["k2", "k16", "kap0", "kap"]),
+}
+PLACE = {name: (buf, i * w, w) for buf, (w, _, names) in PACKS.items() for i, name in enumerate(names)}
+
+
+def _scratch():
+    s = {}
+
+    def sb(d, n, *names):
+        for name in names:
+            s[name] = ("sbuf", [128, n], d)
+
+    def mx(n, *names):
+        for name in names:
+            sb("float8_e4m3fn_x4", n, "q" + name)
+            sb("uint8", n, "s" + name)
+    for buf, (w, d, names) in PACKS.items():
+        sb(d, w * len(names), buf)
+    for t in range(ROUNDS + 1):
+        sb("bfloat16", 1024, "x%d" % t)
+        mx(256, "x%d" % t)
+    for t in range(ROUNDS):
+        mx(256, "l%d" % t, "z%d" % t)
+        sb("int32", 16, "la%d" % t, "xs%d" % t)
+        sb("bfloat16", 1024, "z%d" % t)
+        sb("bfloat16", 512, "w%d" % t)
+        sb("float32", 16, "rs%d" % t)
+        sb("bfloat16", 2048, "h%d" % t)
+    sb("bfloat16", 1024, "zz", "ab", "xh")
+    mx(512, "w", "e")
+    mx(128, "u", "r", "v", "g")
+    for n, k, _ in CTILES:
+        sb("bfloat16", 4 * k, "c" + n)
+        mx(k, "c" + n)
+    sb("bfloat16", 520, "ee")
+    sb("bfloat16", 512, "gj", "gg", "usb", "vsb")
+    sb("bfloat16", 128, "dif")
+    sb("float32", 256, "fd1", "ffw", "ysb")
+    sb("float32", 768, "pw")
+    sb("bfloat16", 256, "t16", "eqk", "fmsk", "d0r", "d0b", "kw", "ibf", "bsum")
+    sb("int32", 256, "prow")
+    sb("int32", 16, "lst0")
+    sb("bfloat16", 1920, "junk", "sgn")
+    sb("int32", 1, "ipcol", "ik", "ig")
+    sb("float32", 1, "fkcol", "fg")
+    sb("int32", 8, "upick")
+    sb("uint16", 8, "u16")
+    sb("uint16", 32, "pq16")
+    for n in ("ps", "ps2", "pc", "pp0", "pp1", "pp2", "pp3"):
+        s[n] = ("psum", [128, 512], "float32")
+    return s
+
+
+SCRATCH = _scratch()
+SEMAPHORES = (["vec", "sca", "ten", "gps", "dx", "du", "dp", "dr", "dw", "dv", "dq", "dy", "dl", "loc"]
+              + ["ca%d" % t for t in range(ROUNDS)] + ["la%d" % t for t in range(ROUNDS)])
+
+
+def rank_program(g, core, T, topo):
+    rank = T.rank_of(core)
+    if rank is None:
+        return
+    n = len(T.cores)
+    nxt, prv = T.cores[(rank + 1) % n], T.cores[(rank - 1) % n]
+    mask = topo.mask(core, nxt)
+    n_out, n_in = len(topo.engines(core, nxt)), len(topo.engines(prv, core))
+    rid, pid = topo.addr(nxt, core)
+    V, S, P, Y = g.vector, g.scalar, g.tensor, g.sync
+    queue = {"v": V, "s": S, "t": P, "g": g, "y": Y}
+    own_sem = {"v": "vec", "s": "sca", "t": "ten", "g": "gps"}
+    count = {"vec": 0, "sca": 0, "ten": 0, "gps": 0, "loc": 0}
+    waited = {}
+    writer, readers = {}, {}
+
+    def W(name, a=0, b=None, step=1):
+        buf, lo, w = PLACE[name]
+        return T[buf][:, lo + a:lo + (w if b is None else b):step]
+
+    def wait(q, tok):
+        sem, val = tok
+        if waited.get((q, sem), 0) < val:
+            queue[q].wait_ge(T.sem[sem], val)
+            waited[(q, sem)] = val
+
+    def order(q, reads, writes, chained=False):
+        need = {}
+        for k in reads:
+            tok = writer[k]
+            need[tok[0]] = max(need.get(tok[0], 0), tok[1])
+        for k in writes:
+            for tok in ([] if chained or k not in writer else [writer[k]]) + [r for r in readers.get(k, []) if r[0] != own_sem.get(q)]:
+                need[tok[0]] = max(need.get(tok[0], 0), tok[1])
+        for sem in need:
+            wait(q, (sem, need[sem]))
+
+    def note(tok, reads, writes):
+        for k in reads:
+            readers.setdefault(k, []).append(tok)
+        for k in writes:
+            writer[k] = tok
+            readers[k] = []
+
+    def do(q, reads, writes, call, chained=False):
+        order(q, reads, writes, chained)
+        sem = own_sem[q]
+        call().then_inc(T.sem[sem], 1)
+        count[sem] += 1
+        note((sem, count[sem]), reads, writes)
+
+    def load(q, buf, out, src, sem, total):
+        queue[q].dma_start(out, src).then_inc(T.sem[sem], 16)
+        note((sem, total), [], [buf])
+
+    def send(out, src, sem, reads):
+        order("g", reads, [])
+        g.remote_dma(out, src, T.sem[sem], T.sem.loc, pid, rid, mask)
+        count["loc"] += n_out
+
+    def tt(out, a, b, op, reads, writes):
+        do("v", reads, writes, lambda: V.tensor_tensor(out, a, b, op))
+
+    def ts(out, a, s1, op0, reads, writes, s2=None, op1=None):
+        if op1 is None:
+            do("v", reads, writes, lambda: V.tensor_scalar(out, a, s1, None, op0))
+        else:
+            do("v", reads, writes, lambda: V.tensor_scalar(out, a, s1, s2, op0, op1))
+
+    def cp(out, a, reads, writes):
+        do("v", reads, writes, lambda: V.tensor_copy(out, a))
+
+    def act(out, a, scale, reads, writes, func=AF.Copy, bias=0.0):
+        if func == AF.Copy:
+            do("s", reads, writes, lambda: S.activation(out, a, func, scale=scale))
+        else:
+            do("s", reads, writes, lambda: S.activation(out, a, func, bias=bias, scale=scale))
+
+    def scan(out, d0, d1, reads, writes, init=0.0, op0=OP.mult, op1=OP.add):
+        do("v", reads, writes, lambda: V.tensor_tensor_scan(out, d0, d1, init, op0, op1))
+
+    def quant(name, tile, reads):
+        do("v", reads, ["q" + name], lambda: V.quantize_mx(T["q" + name][:], T["s" + name][:], tile))
+
+    def fillc(out, value, key):
+        do("v", [], key, lambda: V.memset(out, value))
+
+    def iota(out, pattern, cm, key):
+        do("g", [], [key], lambda: g.iota(out, pattern, 0, cm, allow_small_or_imprecise_dtypes=True))
+
+    def mm(out, a, x, k, reads, writes, start=True, stop=True, col=0, first=0):
+        do("t", reads + ["q" + a, "q" + x], writes,
+           lambda: P.matmul_mx(out, T["q" + a][:, col:col + 128], T["s" + a][:, col:col + 128], T["q" + x][:, first:first + k], T["s" + x][:, first:first + k], start, stop), chained=not start)
+
+    load("y", "x0", T.x0[:], T.x[:], "dx", 16)
+    load("s", "usb", T.usb[:], T.u[:], "du", 16)
+    load("y", "lst0", T.lst0[:], T.p[:], "dp", 16)
+    for r in range(16):
+        load("y", "prow", T.prow[r:128:16, :], T.p[:], "dr", 256)
+    load("y", "qw", T.qw[:].bitcast(dt.uint8), T.wc[:], "dw", 32)
+    load("y", "qw", T.sw[:], T.ws[:], "dw", 32)
+    load("y", "vsb", T.vsb[:], T.v[:], "dv", 16)
+
+    def fill(t):
+        fillc(T["w%d" % t][:, 0:256], 256.0, ["wa%d" % t])
+        fillc(T["w%d" % t][:, 256:512], 0.0, ["wb%d" % t])
+        fillc(T["rs%d" % t][:, 0:1], 0.0, ["rs%d_0" % t])
+
+    def landings(t):
+        return T.lst0[:] if t == 0 else W("lst%d" % t)
+
+    def lists(t):
+        tt(W("own"), W("i1k"), landings(t), OP.add, ["i1k", "lst%d" % t], ["own"])
+        ts(W("lk"), landings(t), 1024.0, OP.mult, ["lst%d" % t], ["lk"])
+        tt(W("neg"), W("ii"), landings(t), OP.subtract, ["ii", "lst%d" % t], ["neg"])
+
+    iota(T.ipcol[:], [[1, 1]], 1, "ipcol")
+    iota(T.t16[:], [[0, 16], [1, 16]], 0, "t16")
+    iota(T.upick[:], [[16, 8]], 0, "upick")
+    iota(W("m16"), [[16, 16]], 0, "m16")
+    iota(W("mm"), [[1, 16]], 0, "mm")
+    iota(T.dif[:], [[1, 128]], -1, "dif")
+    iota(T.gj[:], [[1, 8], [0, 64]], 0, "gj")
+    fillc(T.ee[:], 0.0, ["ee"])
+    ts(T.ik[:], T.ipcol[:], 15, OP.bitwise_and, ["ipcol"], ["ik"])
+    ts(T.ig[:], T.ipcol[:], 4, OP.arith_shift_right, ["ipcol"], ["ig"])
+    cp(T.fkcol[:], T.ik[:], ["ik"], ["fkcol"])
+    ts(W("k2"), T.ik[:], 2.0, OP.add, ["ik"], ["k2"])
+    cp(T.fg[:], T.ig[:], ["ig"], ["fg"])
+    ts(T.eqk[:], T.t16[:], T.fkcol[:, 0:1], OP.is_equal, ["t16", "fkcol"], ["eqk"], 1024.0, OP.mult)
+    cp(T.u16[:], T.upick[:], ["upick"], ["u16"])
+    act(T.d0b[:], T.t16[:], 1.0, ["t16"], ["d0b"], AF.Sign)
+    act(T.d0r[:], T.d0b[:], 2 * BIG, ["d0b"], ["d0r"], AF.Identity, -BIG)
+    act(T.fmsk[:], T.eqk[:], 2 * BIG / 1024, ["eqk"], ["fmsk"], AF.Identity, -BIG)
+    act(W("kwa"), T.t16[:], -1.0, ["t16", "k2"], ["kwa"], AF.Relu, W("k2"))
+    act(W("kwb"), W("kwa"), -LIFT, ["kwa"], ["kwb"], AF.Abs, LIFT - 0.5)
+    for name, k, slots in CTILES:
+        lo = 16 * min(m for m in slots if m != "b")
+        fillc(T["c" + name][:, 4 * lo:4 * k], 0.0, ["c%s%d" % (name, i) for i in range(4)])
+    ts(W("k16"), T.fkcol[:], 16.0, OP.mult, ["fkcol"], ["k16"])
+    ts(W("kap0"), T.fkcol[:], 15.0, OP.is_equal, ["fkcol"], ["kap0"], 1.0 - 1.0 / LIFT, OP.mult)
+    ts(W("r16"), W("m16"), T.fkcol[:, 0:1], OP.subtract, ["m16", "fkcol"], ["r16"], 15.0 - OFF, OP.add)
+    ts(W("ii"), W("m16"), T.fkcol[:, 0:1], OP.add, ["m16", "fkcol"], ["ii"])
+    ts(W("perm"), W("mm"), W("k16"), OP.add, ["mm", "k16"], ["perm"])
+    ts(W("kap"), W("kap0"), 1.0 / LIFT, OP.add, ["kap0"], ["kap"])
+    ts(W("i1k"), W("ii"), -1024.0, OP.mult, ["ii"], ["i1k"])
+    ts(T.ee[:, 4:516:4], T.dif[:], 0.0, OP.is_equal, ["dif"], ["ee"])
+    fill(0)
+    quant("u", T.usb[:], ["usb"])
+    do("v", ["qu", "u16"], ["qr"], lambda: V.tensor_copy(T.qr[:].bitcast(dt.uint32), T.qu[:].bitcast(dt.uint32).indirect(T.u16[:])))
+    do("s", ["qu", "u16"], ["qrs"], lambda: S.activation(T.sr[:], T.su[:].indirect(T.u16[:]), AF.Copy))
+    quant("x0", T.x0[:], ["x0"])
+    act(T.kw[:], W("kwb"), -1.0, ["kwb"], ["kw"], AF.Relu, LIFT + 0.5)
+
+    at = {m: 8 * m * (m - 1) for m in range(1, 16)}
+    views = {}
+    for name, k, slots in CTILES:
+        for i, m in enumerate(slots):
+            if m != "b":
+                views[m] = (T["c" + name][:, i:64 * m:4], "c%s%d" % (name, i))
+
+    for t in range(ROUNDS):
+        last = t == ROUNDS - 1
+        L, Ln, x, xn = "lst%d" % t, "lst%d" % (t + 1), "x%d" % t, "x%d" % (t + 1)
+        h, z, w, rs = T["h%d" % t], T["z%d" % t], T["w%d" % t], T["rs%d" % t]
+        send(T["ql%d" % t][:].bitcast(dt.uint8), T["q" + x][:].bitcast(dt.uint8), "ca%d" % t, ["q" + x])
+        send(T["sl%d" % t][:], T["s" + x][:], "ca%d" % t, ["q" + x])
+        note(("ca%d" % t, 2 * n_in), [], ["ql%d" % t])
+        if t == 0:
+            iota(W("irow"), [[1, 256]], 0, "irow")
+            iota(T.pw[:], [[0, 768]], 0, "pw")
+        mm(T.ps[:, 0:256], "r", x, 256, ["qrs"], ["ps"])
+        mm(T.ps2[:, 0:256], "r", x, 256, ["qrs"], ["ps2"])
+        if t == 0:
+            for b in range(4):
+                do("v", ["ee"], ["qe"], lambda: V.quantize_mx(T.qe[:, 128 * b:128 * b + 128], T.se[:, 128 * b:128 * b + 128], T.ee[:, 4 - b:516 - b]), chained=True)
+        tt(T.fd1[:], T.ps[:, 0:256], T.fmsk[:], OP.min, ["ps", "fmsk"], ["fd1"])
+        scan(T.ffw[:], T.d0r[:], T.fd1[:], ["d0r", "fd1"], ["ffw"], -BIG, OP.min, OP.max)
+        tt(T.ca[:, 0:1024:4], T.ps[:, 0:256], T.ffw[:], OP.is_le, ["ps", "ffw"], ["ca0"])
+
+        def count_row(m, view, key, src, func, reads):
+            do("s", reads, [key, "rs%d_%d" % (t, m)], lambda: S.activation(view, src, func, accum_out=rs[:, m:m + 1]))
+        for m in ON_SCALAR:
+            sg = T.sgn[:, at[m]:at[m] + 16 * m]
+            act(sg, T.ps2[:, 0:16 * m], -1.0, ["ps2", "ffw"], ["sgn%d" % m], AF.Sign, T.ffw[:, 16 * m + 15:16 * m + 16])
+            count_row(m, views[m][0], views[m][1], sg, AF.Relu, ["sgn%d" % m])
+        for ci, (name, k, slots) in enumerate(CTILES):
+            for i, m in enumerate(slots):
+                if m == "b" or m in ON_SCALAR:
+                    continue
+                view, key = views[m]
+                ts(view, T.ps[:, 0:16 * m], T.ffw[:, 16 * m + 15:16 * m + 16], OP.is_lt, ["ps", "ffw"], [key])
+                count_row(m, T.junk[:, at[m]:at[m] + 16 * m], "junk%d" % m, view, AF.Copy, [key])
+            if t == 0 and ci == 0:
+                ts(T.gg[:], T.gj[:], T.fg[:, 0:1], OP.is_equal, ["gj", "fg"], ["gg"])
+                quant("g", T.gg[:], ["gg"])
+            quant("c" + name, T["c" + name][:], ["c%s%d" % (name, i) for i in range(4)])
+            mm(T.pc[:, 0:k], "g", "c" + name, k, [], ["pc"], start=ci == 0, stop=ci == 3)
+        xk = ["x0"] * 4 if t == 0 else ["%s_%d" % (x, b) for b in range(4)]
+        if t == 0:
+            act(W("irs"), W("irow"), 1.0 / 1024.0, ["irow"], ["irs"])
+            act(T.ibf[:], W("irow"), 1.0, ["irow"], ["ibf"])
+        for b in range(4):
+            act(h[:, 512 * b:512 * b + 256], T[x][:, b:1024:4], 0.5, [xk[b]], ["hx%d_%d" % (t, b)])
+        act(T.xh[:], T[x][:], 0.5, xk, ["xh"])
+        for b in range(4):
+            mm(T["pp%d" % b][:, 0:256], "e", "l%d" % t, 256, [], ["pp%d" % b], col=128 * b)
+            act(h[:, 512 * b + 256:512 * b + 512], T["pp%d" % b][:, 0:256], 0.5, ["pp%d" % b], ["hd%d_%d" % (t, b)])
+        scan(T.bsum[:], T.d0b[:], T.ca[:, 0:1024:4], ["d0b", "ca0"], ["bsum"])
+        tt(W("q1"), W("r16"), T.bsum[:, 15:256:16], OP.subtract, ["r16", "bsum"], ["q1"])
+        if t == 0:
+            lists(0)
+            tt(W("vr0"), T.prow[:].indirect(W("perm")), W("irs"), OP.subtract, ["prow", "perm", "irs"], ["vr0"])
+        scan(W("ex"), T.kw[:], T.pc[:, 0:256], ["kw", "pc"], ["ex"])
+        tt(W("q2"), W("q1"), rs[:], OP.subtract, ["q1"] + ["rs%d_%d" % (t, m) for m in range(16)], ["q2"])
+        ts(W("r1"), W("ex", 15, 256, 16), W("kap"), OP.mult, ["ex", "kap"], ["r1"])
+        tt(W("rho"), W("r1"), W("q2"), OP.add, ["r1", "q2"], ["rho"])
+        ts(W("pq", 0, 16), W("rho"), 513.0, OP.mult, ["rho"], ["pqa"])
+        ts(W("pq", 16, 32), W("rho"), 513.0, OP.mult, ["rho"], ["pqb"], 512.0, OP.add)
+        ts(W("pm"), W("pq"), PAIR, OP.bitwise_and, ["pqa", "pqb"], ["pm"])
+        cp(T.pq16[:], W("pm"), ["pm"], ["pq16"])
+        cp(T.pw[:].indirect(T.pq16[:, 0:16]), W("vr%d" % t), ["pq16", "vr%d" % t], ["pw"])
+        tt(W("yy"), T.pw[:].indirect(T.pq16[:, 16:32]), T.eqk[:], OP.mult, ["pw", "pq16", "eqk"], ["yy"])
+        scan(W("fy"), T.d0b[:], W("yy"), ["d0b", "yy"], ["fy"])
+        fy = W("fy", 15, 256, 16)
+        tt(W("ss"), fy, W("own"), OP.add, ["fy", "own"], ["ss"])
+        tt(W("y"), fy, W("lk"), OP.subtract, ["fy", "lk"], ["y"])
+        ts(W("tt"), W("ss"), FIELD, OP.bitwise_and, ["ss"], ["tt"])
+        ts(W("ok"), W("tt"), 0.0, OP.is_equal, ["tt"], ["ok"], 1.0 / 1024.0, OP.mult)
+        tt(W("zl"), W("y"), W("ok"), OP.mult, ["y", "ok"], ["zl"])
+        tt(W(Ln), landings(t), W("zl"), OP.add, [L, "zl"], [Ln])
+        cp(W("l16"), W(Ln), [Ln], ["l16"])
+        cp(w[:, 0:512].indirect(W("l16")), T.ibf[:], ["l16", "ibf"], ["wa%d" % t, "wb%d" % t])
+        scan(W("sx"), T.kw[:], w[:, 256:512], ["kw", "wb%d" % t], ["sx"])
+        ts(T["xs%d" % t][:], W("sx", 15, 256, 16), W("kap"), OP.mult, ["sx", "kap"], ["xs%d" % t], -OFF, OP.add)
+        send(T["la%d" % t][:], T["xs%d" % t][:], "la%d" % t, ["xs%d" % t])
+        note(("la%d" % t, n_in), [], ["la%d" % t])
+        scan(W("so"), T.kw[:], w[:, 0:256], ["kw", "wa%d" % t], ["so"])
+        ts(W("tso"), W("so", 15, 256, 16), W("kap"), OP.mult, ["so", "kap"], ["tso"], -OFF, OP.add)
+        if t == 0:
+            cp(W("lr0"), T.prow[:].indirect(W("perm")), ["prow", "perm"], ["lr0"])
+        ts(W("c1"), W("ss"), 1023, OP.bitwise_and, ["ss"], ["c1"])
+        ts(W("ok1"), W("tt"), 0.0, OP.is_equal, ["tt"], ["ok1"])
+        tt(W("e1"), W("c1"), W("neg"), OP.add, ["c1", "neg"], ["e1"])
+        tt(W("e2"), W("e1"), W("ok1"), OP.mult, ["e1", "ok1"], ["e2"])
+        tt(W("sig"), W("ii"), W("e2"), OP.subtract, ["ii", "e2"], ["sig"])
+        cp(W("sig16"), W("sig"), ["sig"], ["sig16"])
+        lr, lrn = "lr%d" % t, "lr%d" % (t + 1)
+        act(W(lrn), W(lr).indirect(W("sig16")), 1.0, [lr, "sig16"], [lrn])
+        if last:
+            order("y", [lrn], [])
+            lo = PLACE[lrn][1]
+            Y.dma_start(T.ol[:], T.rows[0:128:16, lo:lo + 256]).then_inc(T.sem.dl, 16)
+        else:
+            lists(t + 1)
+            fill(t + 1)
+            tt(W("vr%d" % (t + 1)), W(lrn), W("irs"), OP.subtract, [lrn, "irs"], ["vr%d" % (t + 1)])
+        if t == 0:
+            quant("v", T.vsb[:], ["vsb"])
+        tt(W("its"), W("tso"), T["la%d" % t][:], OP.add, ["tso", "la%d" % t], ["its"])
+        cp(W("ts16"), W("its"), ["its"], ["ts16"])
+        for b in range(4):
+            tt(z[:, b:1024:4], h[:, 512 * b:512 * b + 512].indirect(W("ts16")), T.xh[:, b:1024:4], OP.add,
+               ["ts16", "xh", "hx%d_%d" % (t, b), "hd%d_%d" % (t, b)], ["z%d_%d" % (t, b)])
+            act(T.zz[:, 256 * b:256 * b + 256], z[:, b:1024:4], 32.0, ["z%d_%d" % (t, b)], ["zz%d" % b])
+        quant("z%d" % t, z[:], ["z%d_%d" % (t, b) for b in range(4)])
+        for b in range(4):
+            mm(T["pp%d" % b][:, 0:256], "w", "z%d" % t, 256, [], ["pp%d" % b], col=128 * b)
+        for b in range(4):
+            ab = T.ab[:, 256 * b:256 * b + 256]
+            tt(ab, T["pp%d" % b][:, 0:256], T.zz[:, 256 * b:256 * b + 256], OP.add, ["pp%d" % b, "zz%d" % b], ["ab%d" % b])
+            out = T[xn][:, b:1024:4]
+            if b < 3:
+                act(out, ab, 0.03125, ["ab%d" % b], ["%s_%d" % (xn, b)])
+            else:
+                ts(out, ab, 0.03125, OP.mult, ["ab%d" % b], ["%s_%d" % (xn, b)])
+        quant(xn, T[xn][:], ["%s_%d" % (xn, b) for b in range(4)])
+
+    q = "x%d" % ROUNDS
+    order("y", ["q" + q], [])
+    Y.dma_start(T.oc[:], T["q" + q][:].bitcast(dt.uint8)).then_inc(T.sem.dq, 16)
+    for k in range(4):
+        Y.dma_start(T.osc[4 * k:4 * k + 4, :], T["s" + q][32 * k:32 * k + 4, :]).then_inc(T.sem.dq, 16)
+    mm(T.ps[:, 0:128], "v", q, 128, [], ["ps"])
+    mm(T.ps2[:, 0:128], "v", q, 128, [], ["ps2"], first=128)
+    cp(T.ysb[:, 0:128], T.ps[:, 0:128], ["ps"], ["ysba"])
+    act(T.ysb[:, 128:256], T.ps2[:, 0:128], 1.0, ["ps2"], ["ysbb"])
+    order("y", ["ysba"], [])
+    Y.dma_start(T.y[:, 0:128], T.ysb[:, 0:128]).then_inc(T.sem.dq, 16)
+    order("s", ["ysbb"], [])
+    S.dma_start(T.y[:, 128:256], T.ysb[:, 128:256]).then_inc(T.sem.dy, 16)
+    for sem in ("vec", "sca", "ten", "gps", "loc"):
+        wait("g", (sem, count[sem]))
+    for sem, val in (("dx", 16), ("du", 16), ("dp", 16), ("dr", 256), ("dw", 32), ("dv", 16), ("dq", 96), ("dy", 16), ("dl", 16)):
+        wait("g", (sem, val))
+    for t in range(ROUNDS):
+        wait("g", ("ca%d" % t, 2 * n_in))
+        wait("g", ("la%d" % t, n_in))

@@ -4,21 +4,21 @@ OP = AluOpType
 AF = ActivationFunctionType
 ROUNDS = 3
 BIG = 1e29
-LIFT = 4096.0
-OFF = 0.46875
+LIFT = 1024.0
+SINK = 2048.0
 FIELD = sum(1 << b for b in (8, 9, 18, 19, 20))
 PAIR = 254 + 512
 
-CTILES = [("a", 256, ["b", 15, 14, 13]), ("b", 192, [12, 11, 10, 9]), ("c", 128, [8, 7, 6, 5]), ("d", 128, [4, 3, 2, 1])]
+CTILES = {"a": ("a", 0, 256, ["b", 15, 14, 13]), "b": ("b", 0, 192, [12, 11, 10, 9]), "d": ("b", 192, 64, [4, 3, 2, 1]), "c": ("c", 0, 128, [8, 7, 6, 5])}
 ON_SCALAR = [15, 12]
 
 PACKS = {
-    "rows": (256, "float32", ["irow", "irs", "ex", "yy", "fy", "sx", "so", "vr0", "vr1", "vr2", "lr0", "lr1", "lr2", "lr3", "kwa", "kwb"]),
-    "flist": (16, "float32", ["r16", "q1", "q2", "r1", "ok", "ok1", "y", "zl", "e1", "e2", "own", "neg", "lk", "i1k"]),
-    "ilist": (16, "int32", ["m16", "mm", "ii", "ss", "tt", "c1", "rho", "sig", "tso", "its", "lst1", "lst2", "lst3"]),
+    "rows": (256, "float32", ["irs", "ex", "yy", "fy", "sw", "vr", "lr"]),
+    "flist": (16, "float32", ["r16", "q1", "own", "lk", "i1k", "rs"]),
+    "ilist": (16, "int32", ["m16", "m16r", "ss", "tt"]),
     "iwide": (32, "int32", ["pq", "pm"]),
-    "ulist": (16, "uint16", ["perm", "l16", "sig16", "ts16"]),
-    "cols": (1, "float32", ["k2", "k16", "kap0", "kap"]),
+    "fwide": (32, "float32", ["mz", "md", "mo"]),
+    "cols": (1, "float32", ["k2", "e15", "offk"]),
 }
 PLACE = {name: (buf, i * w, w) for buf, (w, _, names) in PACKS.items() for i, name in enumerate(names)}
 
@@ -39,40 +39,43 @@ def _scratch():
     for t in range(ROUNDS + 1):
         sb("bfloat16", 1024, "x%d" % t)
         mx(256, "x%d" % t)
+        sb("uint16", 16, "ls%d" % t)
     for t in range(ROUNDS):
         mx(256, "l%d" % t, "z%d" % t)
-        sb("int32", 16, "la%d" % t, "xs%d" % t)
+        sb("uint16", 16, "la%d" % t)
         sb("bfloat16", 1024, "z%d" % t)
-        sb("bfloat16", 512, "w%d" % t)
-        sb("float32", 16, "rs%d" % t)
         sb("bfloat16", 2048, "h%d" % t)
-    sb("bfloat16", 1024, "zz", "ab", "xh")
+    sb("bfloat16", 1024, "zz", "ab", "xh", "ca")
+    sb("bfloat16", 1280, "cb")
     mx(512, "w", "e")
-    mx(128, "u", "r", "v", "g")
-    for n, k, _ in CTILES:
-        sb("bfloat16", 4 * k, "c" + n)
-        mx(k, "c" + n)
+    mx(128, "u", "r", "v", "g", "cc")
+    mx(256, "ca")
+    mx(320, "cb")
     sb("bfloat16", 520, "ee")
-    sb("bfloat16", 512, "gj", "gg", "usb", "vsb")
+    sb("bfloat16", 512, "gj", "gg", "usb", "vsb", "cc")
     sb("bfloat16", 128, "dif")
     sb("float32", 256, "fd1", "ffw", "ysb")
+    sb("float32", 272, "kwa", "kwb", "ctl")
+    sb("float32", 512, "irow")
     sb("float32", 768, "pw")
-    sb("bfloat16", 256, "t16", "eqk", "fmsk", "d0r", "d0b", "kw", "ibf", "bsum")
-    sb("int32", 256, "prow")
+    sb("bfloat16", 768, "w")
+    sb("bfloat16", 272, "t16")
+    sb("bfloat16", 256, "eqk", "fmsk", "d0r", "d0b", "ibf", "ibn", "bsum")
     sb("int32", 16, "lst0")
     sb("bfloat16", 1920, "junk", "sgn")
     sb("int32", 1, "ipcol", "ik", "ig")
     sb("float32", 1, "fkcol", "fg")
     sb("int32", 8, "upick")
     sb("uint16", 8, "u16")
+    sb("uint16", 16, "ts16")
     sb("uint16", 32, "pq16")
-    for n in ("ps", "ps2", "pc", "pp0", "pp1", "pp2", "pp3"):
-        s[n] = ("psum", [128, 512], "float32")
+    for b in range(8):
+        s["pb%d" % b] = ("psum", [128, 512], "float32")
     return s
 
 
 SCRATCH = _scratch()
-SEMAPHORES = (["vec", "sca", "ten", "gps", "dx", "du", "dp", "dr", "dw", "dv", "dq", "dy", "dl", "loc"]
+SEMAPHORES = (["vec", "sca", "ten", "gps", "dx0", "dx1", "du", "dp", "dw", "dv", "dq", "dy", "dl", "loc"]
               + ["ca%d" % t for t in range(ROUNDS)] + ["la%d" % t for t in range(ROUNDS)])
 
 
@@ -157,219 +160,265 @@ def rank_program(g, core, T, topo):
     def scan(out, d0, d1, reads, writes, init=0.0, op0=OP.mult, op1=OP.add):
         do("v", reads, writes, lambda: V.tensor_tensor_scan(out, d0, d1, init, op0, op1))
 
-    def quant(name, tile, reads):
-        do("v", reads, ["q" + name], lambda: V.quantize_mx(T["q" + name][:], T["s" + name][:], tile))
+    def quant(name, tile, reads, a=0, b=None, key=None):
+        b = T["q" + name].shape[1] if b is None else b
+        do("v", reads, [key or "q" + name], lambda: V.quantize_mx(T["q" + name][:, a:b], T["s" + name][:, a:b], tile[:, 4 * a:4 * b]))
 
     def fillc(out, value, key):
         do("v", [], key, lambda: V.memset(out, value))
 
-    def iota(out, pattern, cm, key):
-        do("g", [], [key], lambda: g.iota(out, pattern, 0, cm, allow_small_or_imprecise_dtypes=True))
+    def iota(out, pattern, cm, key, base=0):
+        do("g", [], [key], lambda: g.iota(out, pattern, base, cm, allow_small_or_imprecise_dtypes=True))
 
-    def mm(out, a, x, k, reads, writes, start=True, stop=True, col=0, first=0):
-        do("t", reads + ["q" + a, "q" + x], writes,
-           lambda: P.matmul_mx(out, T["q" + a][:, col:col + 128], T["s" + a][:, col:col + 128], T["q" + x][:, first:first + k], T["s" + x][:, first:first + k], start, stop), chained=not start)
+    def mm(bank, a, x, k, reads, start=True, stop=True, col=0, first=0):
+        do("t", reads, ["pb%d" % bank],
+           lambda: P.matmul_mx(T["pb%d" % bank][:, 0:k], T["q" + a][:, col:col + 128], T["s" + a][:, col:col + 128], T["q" + x][:, first:first + k], T["s" + x][:, first:first + k], start, stop), chained=not start)
 
-    load("y", "x0", T.x0[:], T.x[:], "dx", 16)
+    load("y", "x0_0", T.x0[:, 0:512], T.x[:, 0:512], "dx0", 16)
     load("s", "usb", T.usb[:], T.u[:], "du", 16)
+    load("y", "x0_1", T.x0[:, 512:1024], T.x[:, 512:1024], "dx1", 16)
     load("y", "lst0", T.lst0[:], T.p[:], "dp", 16)
-    for r in range(16):
-        load("y", "prow", T.prow[r:128:16, :], T.p[:], "dr", 256)
     load("y", "qw", T.qw[:].bitcast(dt.uint8), T.wc[:], "dw", 32)
     load("y", "qw", T.sw[:], T.ws[:], "dw", 32)
     load("y", "vsb", T.vsb[:], T.v[:], "dv", 16)
 
-    def fill(t):
-        fillc(T["w%d" % t][:, 0:256], 256.0, ["wa%d" % t])
-        fillc(T["w%d" % t][:, 256:512], 0.0, ["wb%d" % t])
-        fillc(T["rs%d" % t][:, 0:1], 0.0, ["rs%d_0" % t])
-
-    def landings(t):
-        return T.lst0[:] if t == 0 else W("lst%d" % t)
-
     def lists(t):
-        tt(W("own"), W("i1k"), landings(t), OP.add, ["i1k", "lst%d" % t], ["own"])
-        ts(W("lk"), landings(t), 1024.0, OP.mult, ["lst%d" % t], ["lk"])
-        tt(W("neg"), W("ii"), landings(t), OP.subtract, ["ii", "lst%d" % t], ["neg"])
+        ls = "ls%d" % t
+        cp(W("md", 1, 32, 2), T[ls][:], [ls], ["lf"])
+        ts(W("lk"), T[ls][:], 1024.0, OP.mult, [ls], ["lk"])
+        return lambda: tt(W("own"), W("i1k"), W("md", 1, 32, 2), OP.add, ["i1k", "lf"], ["own"])
+
+    def packed_row(t):
+        tt(W("vr"), T.irow[:].indirect(T["ls%d" % t][:]), W("irs"), OP.subtract, ["irow", "ls%d" % t, "irs"], ["vr"])
 
     iota(T.ipcol[:], [[1, 1]], 1, "ipcol")
-    iota(T.t16[:], [[0, 16], [1, 16]], 0, "t16")
     iota(T.upick[:], [[16, 8]], 0, "upick")
-    iota(W("m16"), [[16, 16]], 0, "m16")
-    iota(W("mm"), [[1, 16]], 0, "mm")
-    iota(T.dif[:], [[1, 128]], -1, "dif")
+    iota(T.t16[:], [[0, 17], [1, 16]], 0, "t16")
     iota(T.gj[:], [[1, 8], [0, 64]], 0, "gj")
-    fillc(T.ee[:], 0.0, ["ee"])
+    iota(W("m16"), [[16, 16]], 0, "m16")
+    iota(W("m16r"), [[16, 16]], 0, "m16r", 15 - 256 - int(SINK))
+    iota(T.dif[:], [[1, 128]], -1, "dif")
+    iota(T.irow[:], [[1, 512]], 0, "irow")
+    fillc(T.ca[:, 4 * 208:1024], 0.0, ["ca%d" % i for i in range(4)])
     ts(T.ik[:], T.ipcol[:], 15, OP.bitwise_and, ["ipcol"], ["ik"])
     ts(T.ig[:], T.ipcol[:], 4, OP.arith_shift_right, ["ipcol"], ["ig"])
+    fillc(T.cb[:, 4 * 144:1280], 0.0, ["cb%d" % i for i in range(4)] + ["cd%d" % i for i in range(4)])
     cp(T.fkcol[:], T.ik[:], ["ik"], ["fkcol"])
     ts(W("k2"), T.ik[:], 2.0, OP.add, ["ik"], ["k2"])
-    cp(T.fg[:], T.ig[:], ["ig"], ["fg"])
-    ts(T.eqk[:], T.t16[:], T.fkcol[:, 0:1], OP.is_equal, ["t16", "fkcol"], ["eqk"], 1024.0, OP.mult)
     cp(T.u16[:], T.upick[:], ["upick"], ["u16"])
-    act(T.d0b[:], T.t16[:], 1.0, ["t16"], ["d0b"], AF.Sign)
-    act(T.d0r[:], T.d0b[:], 2 * BIG, ["d0b"], ["d0r"], AF.Identity, -BIG)
+    cp(T.fg[:], T.ig[:], ["ig"], ["fg"])
+    ts(W("e15"), T.fkcol[:], 15.0, OP.is_equal, ["fkcol"], ["e15"], LIFT, OP.mult)
+    fillc(T.cc[:, 4 * 80:512], 0.0, ["cc%d" % i for i in range(4)])
+    ts(T.eqk[:], T.t16[:, 0:256], T.fkcol[:, 0:1], OP.is_equal, ["t16", "fkcol"], ["eqk"], 1024.0, OP.mult)
+    ts(W("offk"), W("e15"), 256.0 - LIFT, OP.add, ["e15"], ["offk"])
+    quant("cb", T.cb, ["cb0"], 192, 320, "qcz")
+    fillc(W("rs", 0, 1), 0.0, ["rs0"])
+    fillc(W("mz"), 0.0, ["ok"])
+    fillc(T.ee[:], 0.0, ["ee"])
+    act(T.d0b[:], T.t16[:, 0:256], 1.0, ["t16"], ["d0b"], AF.Sign)
     act(T.fmsk[:], T.eqk[:], 2 * BIG / 1024, ["eqk"], ["fmsk"], AF.Identity, -BIG)
-    act(W("kwa"), T.t16[:], -1.0, ["t16", "k2"], ["kwa"], AF.Relu, W("k2"))
-    act(W("kwb"), W("kwa"), -LIFT, ["kwa"], ["kwb"], AF.Abs, LIFT - 0.5)
-    for name, k, slots in CTILES:
-        lo = 16 * min(m for m in slots if m != "b")
-        fillc(T["c" + name][:, 4 * lo:4 * k], 0.0, ["c%s%d" % (name, i) for i in range(4)])
-    ts(W("k16"), T.fkcol[:], 16.0, OP.mult, ["fkcol"], ["k16"])
-    ts(W("kap0"), T.fkcol[:], 15.0, OP.is_equal, ["fkcol"], ["kap0"], 1.0 - 1.0 / LIFT, OP.mult)
-    ts(W("r16"), W("m16"), T.fkcol[:, 0:1], OP.subtract, ["m16", "fkcol"], ["r16"], 15.0 - OFF, OP.add)
-    ts(W("ii"), W("m16"), T.fkcol[:, 0:1], OP.add, ["m16", "fkcol"], ["ii"])
-    ts(W("perm"), W("mm"), W("k16"), OP.add, ["mm", "k16"], ["perm"])
-    ts(W("kap"), W("kap0"), 1.0 / LIFT, OP.add, ["kap0"], ["kap"])
-    ts(W("i1k"), W("ii"), -1024.0, OP.mult, ["ii"], ["i1k"])
-    ts(T.ee[:, 4:516:4], T.dif[:], 0.0, OP.is_equal, ["dif"], ["ee"])
-    fill(0)
-    quant("u", T.usb[:], ["usb"])
+    act(T.d0r[:], T.d0b[:], 2 * BIG, ["d0b"], ["d0r"], AF.Identity, -BIG)
+    quant("u", T.usb, ["usb"])
     do("v", ["qu", "u16"], ["qr"], lambda: V.tensor_copy(T.qr[:].bitcast(dt.uint32), T.qu[:].bitcast(dt.uint32).indirect(T.u16[:])))
     do("s", ["qu", "u16"], ["qrs"], lambda: S.activation(T.sr[:], T.su[:].indirect(T.u16[:]), AF.Copy))
-    quant("x0", T.x0[:], ["x0"])
-    act(T.kw[:], W("kwb"), -1.0, ["kwb"], ["kw"], AF.Relu, LIFT + 0.5)
+    act(T.kwa[:], T.t16[:], -1.0, ["t16", "k2"], ["kwa"], AF.Relu, W("k2"))
+    act(T.kwb[:], T.kwa[:], 7 * LIFT, ["kwa"], ["kwb"], AF.Abs, -4 * LIFT)
 
     at = {m: 8 * m * (m - 1) for m in range(1, 16)}
     views = {}
-    for name, k, slots in CTILES:
+    for name, (buf, c0, k, slots) in CTILES.items():
         for i, m in enumerate(slots):
             if m != "b":
-                views[m] = (T["c" + name][:, i:64 * m:4], "c%s%d" % (name, i))
+                views[m] = (T["c" + buf][:, 4 * c0 + i:4 * c0 + 64 * m:4], "c%s%d" % (name, i))
+    slot_keys = {name: ["c%s%d" % (name, i) for i in range(4)] for name in CTILES}
+    V0, VF, SF, PC = 0, 2, 3, 4
+    UNPACK = [5, 6, 7, 1]
 
+    def latch(hf, bank, lo):
+        cols = slice(128 * hf, 128 * hf + 128)
+        first = lambda: tt(T.fd1[:, cols], T["pb%d" % bank][:, lo:lo + 128], T.fmsk[:, cols], OP.min, ["pb%d" % bank, "fmsk"], ["fd%d" % hf])
+        second = lambda: scan(T.ffw[:, cols], T.d0r[:, cols], T.fd1[:, cols], ["d0r", "fd%d" % hf], ["ffw%d" % hf], -BIG, OP.min, OP.max)
+        return first, second
+
+    def row(m):
+        bank = V0 if m <= 8 else VF
+        view, key = views[m]
+        ts(view, T["pb%d" % bank][:, 0:16 * m], T.ffw[:, 16 * m + 15:16 * m + 16], OP.is_lt, ["pb%d" % bank, "ffw%d" % (m // 8)], [key])
+
+    def count_row(m):
+        view, key = views[m]
+        if m in ON_SCALAR:
+            do("s", ["sgn%d" % m], [key, "rs%d" % m], lambda: S.activation(view, T.sgn[:, at[m]:at[m] + 16 * m], AF.Relu, accum_out=W("rs", m, m + 1)))
+        else:
+            do("s", [key], ["junk%d" % m, "rs%d" % m], lambda: S.activation(T.junk[:, at[m]:at[m] + 16 * m], view, AF.Copy, accum_out=W("rs", m, m + 1)))
+
+    def sign_row(m):
+        act(T.sgn[:, at[m]:at[m] + 16 * m], T["pb%d" % SF][:, 0:16 * m], -1.0, ["pb%d" % SF, "ffw%d" % (m // 8)], ["sgn%d" % m], AF.Sign, T.ffw[:, 16 * m + 15:16 * m + 16])
+
+    def scores_first(x):
+        quant(x, T[x], [x + "_0"], 0, 128, "q%s_0" % x)
+        mm(V0, "r", x, 128, ["qr", "qrs", "q%s_0" % x])
+
+    scores_first("x0")
     for t in range(ROUNDS):
         last = t == ROUNDS - 1
-        L, Ln, x, xn = "lst%d" % t, "lst%d" % (t + 1), "x%d" % t, "x%d" % (t + 1)
-        h, z, w, rs = T["h%d" % t], T["z%d" % t], T["w%d" % t], T["rs%d" % t]
-        send(T["ql%d" % t][:].bitcast(dt.uint8), T["q" + x][:].bitcast(dt.uint8), "ca%d" % t, ["q" + x])
-        send(T["sl%d" % t][:], T["s" + x][:], "ca%d" % t, ["q" + x])
+        x, xn, ls, la = "x%d" % t, "x%d" % (t + 1), "ls%d" % (t + 1), "la%d" % t
+        h, z = T["h%d" % t], T["z%d" % t]
+        qx = ["q%s_0" % x, "q%s_1" % x]
+        min0, scan0 = latch(0, V0, 0)
+        min1, scan1 = latch(1, VF, 128)
+        quant(x, T[x], [x + "_1"], 128, 256, qx[1])
+        mm(VF, "r", x, 256, qx)
+        mm(SF, "r", x, 256, qx)
+        if t > 0:
+            lists(t)()
+            min0()
+        send(T["ql%d" % t][:].bitcast(dt.uint8), T["q" + x][:].bitcast(dt.uint8), "ca%d" % t, qx)
+        send(T["sl%d" % t][:], T["s" + x][:], "ca%d" % t, qx)
         note(("ca%d" % t, 2 * n_in), [], ["ql%d" % t])
         if t == 0:
-            iota(W("irow"), [[1, 256]], 0, "irow")
-            iota(T.pw[:], [[0, 768]], 0, "pw")
-        mm(T.ps[:, 0:256], "r", x, 256, ["qrs"], ["ps"])
-        mm(T.ps2[:, 0:256], "r", x, 256, ["qrs"], ["ps2"])
+            ts(T.gg[:], T.gj[:], T.fg[:, 0:1], OP.is_equal, ["gj", "fg"], ["gg"])
+            min0()
+            quant("g", T.gg, ["gg"])
+            act(T.ctl[:], T.kwb[:], -1.0, ["kwb"], ["ctl"], AF.Identity, 4 * LIFT)
+        scan0()
         if t == 0:
-            for b in range(4):
-                do("v", ["ee"], ["qe"], lambda: V.quantize_mx(T.qe[:, 128 * b:128 * b + 128], T.se[:, 128 * b:128 * b + 128], T.ee[:, 4 - b:516 - b]), chained=True)
-        tt(T.fd1[:], T.ps[:, 0:256], T.fmsk[:], OP.min, ["ps", "fmsk"], ["fd1"])
-        scan(T.ffw[:], T.d0r[:], T.fd1[:], ["d0r", "fd1"], ["ffw"], -BIG, OP.min, OP.max)
-        tt(T.ca[:, 0:1024:4], T.ps[:, 0:256], T.ffw[:], OP.is_le, ["ps", "ffw"], ["ca0"])
-
-        def count_row(m, view, key, src, func, reads):
-            do("s", reads, [key, "rs%d_%d" % (t, m)], lambda: S.activation(view, src, func, accum_out=rs[:, m:m + 1]))
-        for m in ON_SCALAR:
-            sg = T.sgn[:, at[m]:at[m] + 16 * m]
-            act(sg, T.ps2[:, 0:16 * m], -1.0, ["ps2", "ffw"], ["sgn%d" % m], AF.Sign, T.ffw[:, 16 * m + 15:16 * m + 16])
-            count_row(m, views[m][0], views[m][1], sg, AF.Relu, ["sgn%d" % m])
-        for ci, (name, k, slots) in enumerate(CTILES):
-            for i, m in enumerate(slots):
-                if m == "b" or m in ON_SCALAR:
-                    continue
-                view, key = views[m]
-                ts(view, T.ps[:, 0:16 * m], T.ffw[:, 16 * m + 15:16 * m + 16], OP.is_lt, ["ps", "ffw"], [key])
-                count_row(m, T.junk[:, at[m]:at[m] + 16 * m], "junk%d" % m, view, AF.Copy, [key])
-            if t == 0 and ci == 0:
-                ts(T.gg[:], T.gj[:], T.fg[:, 0:1], OP.is_equal, ["gj", "fg"], ["gg"])
-                quant("g", T.gg[:], ["gg"])
-            quant("c" + name, T["c" + name][:], ["c%s%d" % (name, i) for i in range(4)])
-            mm(T.pc[:, 0:k], "g", "c" + name, k, [], ["pc"], start=ci == 0, stop=ci == 3)
-        xk = ["x0"] * 4 if t == 0 else ["%s_%d" % (x, b) for b in range(4)]
-        if t == 0:
-            act(W("irs"), W("irow"), 1.0 / 1024.0, ["irow"], ["irs"])
-            act(T.ibf[:], W("irow"), 1.0, ["irow"], ["ibf"])
-        for b in range(4):
-            act(h[:, 512 * b:512 * b + 256], T[x][:, b:1024:4], 0.5, [xk[b]], ["hx%d_%d" % (t, b)])
-        act(T.xh[:], T[x][:], 0.5, xk, ["xh"])
-        for b in range(4):
-            mm(T["pp%d" % b][:, 0:256], "e", "l%d" % t, 256, [], ["pp%d" % b], col=128 * b)
-            act(h[:, 512 * b + 256:512 * b + 512], T["pp%d" % b][:, 0:256], 0.5, ["pp%d" % b], ["hd%d_%d" % (t, b)])
+            ts(W("r16"), W("m16r"), T.fkcol[:, 0:1], OP.subtract, ["m16r", "fkcol", "offk"], ["r16"], W("offk"), OP.add)
+            ts(W("i1k"), W("m16"), T.fkcol[:, 0:1], OP.add, ["m16", "fkcol"], ["i1k"], -1024.0, OP.mult)
+        for m in (7, 6, 5, 4):
+            row(m)
+        for m in (7, 6, 5):
+            count_row(m)
+        min1()
+        row(3)
+        row(2)
+        scan1()
+        row(1)
+        sign_row(15)
+        count_row(4)
+        count_row(15)
+        sign_row(12)
+        count_row(3)
+        count_row(12)
+        count_row(2)
+        count_row(1)
+        tt(T.ca[:, 0:1024:4], T["pb%d" % VF][:, 0:256], T.ffw[:], OP.is_le, ["pb%d" % VF, "ffw0", "ffw1"], ["ca0"])
+        for m in (14, 13, 11):
+            row(m)
+            count_row(m)
+        quant("ca", T.ca, slot_keys["a"])
+        mm(PC, "g", "ca", 256, ["qg", "qca"], True, False)
+        for m in (10, 9, 8):
+            row(m)
+            count_row(m)
+        quant("cb", T.cb, slot_keys["b"] + slot_keys["d"] + ["qcz"], 0, 256)
+        mm(PC, "g", "cb", 192, ["qcb"], False, False)
+        mm(PC, "g", "cb", 128, ["qcb"], False, False, first=192)
+        quant("cc", T.cc, slot_keys["c"])
+        mm(PC, "g", "cc", 128, ["qcc"], False, True)
         scan(T.bsum[:], T.d0b[:], T.ca[:, 0:1024:4], ["d0b", "ca0"], ["bsum"])
+        if t == 0:
+            cp(T.ls0[:], T.lst0[:], ["lst0"], ["ls0"])
+            act(W("irs"), T.irow[:, 0:256], 1.0 / 1024.0, ["irow"], ["irs"])
+            act(T.pw[:, 0:512], T.irow[:], 1.0, ["irow"], ["pw"])
+            act(T.pw[:, 512:768], T.irow[:, 0:256], 1.0, ["irow"], ["pw"])
         tt(W("q1"), W("r16"), T.bsum[:, 15:256:16], OP.subtract, ["r16", "bsum"], ["q1"])
         if t == 0:
-            lists(0)
-            tt(W("vr0"), T.prow[:].indirect(W("perm")), W("irs"), OP.subtract, ["prow", "perm", "irs"], ["vr0"])
-        scan(W("ex"), T.kw[:], T.pc[:, 0:256], ["kw", "pc"], ["ex"])
-        tt(W("q2"), W("q1"), rs[:], OP.subtract, ["q1"] + ["rs%d_%d" % (t, m) for m in range(16)], ["q2"])
-        ts(W("r1"), W("ex", 15, 256, 16), W("kap"), OP.mult, ["ex", "kap"], ["r1"])
-        tt(W("rho"), W("r1"), W("q2"), OP.add, ["r1", "q2"], ["rho"])
-        ts(W("pq", 0, 16), W("rho"), 513.0, OP.mult, ["rho"], ["pqa"])
-        ts(W("pq", 16, 32), W("rho"), 513.0, OP.mult, ["rho"], ["pqb"], 512.0, OP.add)
+            ts(T.ee[:, 4:516:4], T.dif[:], 0.0, OP.is_equal, ["dif"], ["ee"])
+        tt(T.ctl[:, 16:272:16], W("q1"), W("rs"), OP.subtract, ["q1"] + ["rs%d" % m for m in range(16)], ["ctl"])
+        if t == 0:
+            own0 = lists(0)
+        scan(W("ex"), T["pb%d" % PC][:, 0:256], T.ctl[:, 1:257], ["ctl", "pb%d" % PC], ["ex"], 0.0, OP.max, OP.add)
+
+        def unpacker(b):
+            if t == 0:
+                do("v", ["ee"], ["qe%d" % b], lambda: V.quantize_mx(T.qe[:, 128 * b:128 * b + 128], T.se[:, 128 * b:128 * b + 128], T.ee[:, 4 - b:516 - b]))
+        if t == 0:
+            packed_row(0)
+        ex = W("ex", 15, 256, 16)
+        ts(W("pq", 0, 16), ex, SINK, OP.add, ["ex"], ["pqa"], 513.0, OP.mult)
+        ts(W("pq", 16, 32), ex, 513.0, OP.mult, ["ex"], ["pqb"], 513.0 * SINK + 512.0, OP.add)
+        if t == 0:
+            own0()
         ts(W("pm"), W("pq"), PAIR, OP.bitwise_and, ["pqa", "pqb"], ["pm"])
+        unpacker(0)
         cp(T.pq16[:], W("pm"), ["pm"], ["pq16"])
-        cp(T.pw[:].indirect(T.pq16[:, 0:16]), W("vr%d" % t), ["pq16", "vr%d" % t], ["pw"])
+        unpacker(1)
+        cp(T.pw[:].indirect(T.pq16[:, 0:16]), W("vr"), ["pq16", "vr"], ["pw"])
+        unpacker(2)
         tt(W("yy"), T.pw[:].indirect(T.pq16[:, 16:32]), T.eqk[:], OP.mult, ["pw", "pq16", "eqk"], ["yy"])
+        unpacker(3)
+        if t == 0:
+            act(T.ibf[:], T.irow[:, 0:256], 1.0, ["irow"], ["ibf"])
+            act(T.ibn[:], T.irow[:, 0:256], 1.0, ["irow"], ["ibn"], AF.Identity, -256.0)
+            act(T.w[:, 0:512], T.irow[:], 0.0, ["irow"], ["w"])
+            act(T.w[:, 512:768], T.irow[:, 0:256], 0.0, ["irow"], ["w"])
+        for b in range(4):
+            act(h[:, 512 * b + 256:512 * b + 512], T[x][:, b:1024:4], 0.5, [x + "_0", x + "_1"], ["hx%d_%d" % (t, b)])
+        act(T.xh[:], T[x][:], 0.5, [x + "_0", x + "_1"], ["xh"])
+        for b in range(4):
+            mm(UNPACK[b], "e", "l%d" % t, 256, ["qe%d" % b, "ql%d" % t], col=128 * b)
+            act(h[:, 512 * b:512 * b + 256], T["pb%d" % UNPACK[b]][:, 0:256], 0.5, ["pb%d" % UNPACK[b]], ["hd%d_%d" % (t, b)])
         scan(W("fy"), T.d0b[:], W("yy"), ["d0b", "yy"], ["fy"])
         fy = W("fy", 15, 256, 16)
         tt(W("ss"), fy, W("own"), OP.add, ["fy", "own"], ["ss"])
-        tt(W("y"), fy, W("lk"), OP.subtract, ["fy", "lk"], ["y"])
+        tt(W("md", 0, 32, 2), fy, W("lk"), OP.subtract, ["fy", "lk"], ["y"])
         ts(W("tt"), W("ss"), FIELD, OP.bitwise_and, ["ss"], ["tt"])
-        ts(W("ok"), W("tt"), 0.0, OP.is_equal, ["tt"], ["ok"], 1.0 / 1024.0, OP.mult)
-        tt(W("zl"), W("y"), W("ok"), OP.mult, ["y", "ok"], ["zl"])
-        tt(W(Ln), landings(t), W("zl"), OP.add, [L, "zl"], [Ln])
-        cp(W("l16"), W(Ln), [Ln], ["l16"])
-        cp(w[:, 0:512].indirect(W("l16")), T.ibf[:], ["l16", "ibf"], ["wa%d" % t, "wb%d" % t])
-        scan(W("sx"), T.kw[:], w[:, 256:512], ["kw", "wb%d" % t], ["sx"])
-        ts(T["xs%d" % t][:], W("sx", 15, 256, 16), W("kap"), OP.mult, ["sx", "kap"], ["xs%d" % t], -OFF, OP.add)
-        send(T["la%d" % t][:], T["xs%d" % t][:], "la%d" % t, ["xs%d" % t])
-        note(("la%d" % t, n_in), [], ["la%d" % t])
-        scan(W("so"), T.kw[:], w[:, 0:256], ["kw", "wa%d" % t], ["so"])
-        ts(W("tso"), W("so", 15, 256, 16), W("kap"), OP.mult, ["so", "kap"], ["tso"], -OFF, OP.add)
-        if t == 0:
-            cp(W("lr0"), T.prow[:].indirect(W("perm")), ["prow", "perm"], ["lr0"])
-        ts(W("c1"), W("ss"), 1023, OP.bitwise_and, ["ss"], ["c1"])
-        ts(W("ok1"), W("tt"), 0.0, OP.is_equal, ["tt"], ["ok1"])
-        tt(W("e1"), W("c1"), W("neg"), OP.add, ["c1", "neg"], ["e1"])
-        tt(W("e2"), W("e1"), W("ok1"), OP.mult, ["e1", "ok1"], ["e2"])
-        tt(W("sig"), W("ii"), W("e2"), OP.subtract, ["ii", "e2"], ["sig"])
-        cp(W("sig16"), W("sig"), ["sig"], ["sig16"])
-        lr, lrn = "lr%d" % t, "lr%d" % (t + 1)
-        act(W(lrn), W(lr).indirect(W("sig16")), 1.0, [lr, "sig16"], [lrn])
+        ts(W("mz", 1, 32, 2), W("tt"), 0.0, OP.is_equal, ["tt"], ["ok"], 1.0 / 1024.0, OP.mult)
+        scan(W("mo"), W("mz"), W("md"), ["ok", "y", "lf"], ["mo"])
+        ts(T[ls][:], W("mo", 1, 32, 2), 0.25, OP.add, ["mo"], [ls])
+        send(T[la][:], T[ls][:], la, [ls])
+        note((la, n_in), [], [la])
+        cp(T.w[:, 256:768].indirect(T[ls][:]), T.ibf[:], [ls, "ibf"], ["w"])
         if last:
-            order("y", [lrn], [])
-            lo = PLACE[lrn][1]
+            act(W("lr"), T.irow[:].indirect(T[ls][:]), 1.0, ["irow", ls], ["lr"])
+            order("y", ["lr"], [])
+            lo = PLACE["lr"][1]
             Y.dma_start(T.ol[:], T.rows[0:128:16, lo:lo + 256]).then_inc(T.sem.dl, 16)
         else:
-            lists(t + 1)
-            fill(t + 1)
-            tt(W("vr%d" % (t + 1)), W(lrn), W("irs"), OP.subtract, [lrn, "irs"], ["vr%d" % (t + 1)])
+            packed_row(t + 1)
         if t == 0:
-            quant("v", T.vsb[:], ["vsb"])
-        tt(W("its"), W("tso"), T["la%d" % t][:], OP.add, ["tso", "la%d" % t], ["its"])
-        cp(W("ts16"), W("its"), ["its"], ["ts16"])
+            quant("v", T.vsb, ["vsb"])
+        cp(T.w[:, 0:512].indirect(T[la][:]), T.ibn[:], [la, "ibn"], ["w"])
+        scan(W("sw"), T.ctl[:, 0:256], T.w[:, 256:512], ["ctl", "w"], ["sw"], 0.0, OP.add, OP.max)
+        ts(T.ts16[:], W("sw", 15, 256, 16), W("offk"), OP.add, ["sw", "offk"], ["ts16"])
         for b in range(4):
-            tt(z[:, b:1024:4], h[:, 512 * b:512 * b + 512].indirect(W("ts16")), T.xh[:, b:1024:4], OP.add,
+            tt(z[:, b:1024:4], h[:, 512 * b:512 * b + 512].indirect(T.ts16[:]), T.xh[:, b:1024:4], OP.add,
                ["ts16", "xh", "hx%d_%d" % (t, b), "hd%d_%d" % (t, b)], ["z%d_%d" % (t, b)])
             act(T.zz[:, 256 * b:256 * b + 256], z[:, b:1024:4], 32.0, ["z%d_%d" % (t, b)], ["zz%d" % b])
-        quant("z%d" % t, z[:], ["z%d_%d" % (t, b) for b in range(4)])
-        for b in range(4):
-            mm(T["pp%d" % b][:, 0:256], "w", "z%d" % t, 256, [], ["pp%d" % b], col=128 * b)
-        for b in range(4):
-            ab = T.ab[:, 256 * b:256 * b + 256]
-            tt(ab, T["pp%d" % b][:, 0:256], T.zz[:, 256 * b:256 * b + 256], OP.add, ["pp%d" % b, "zz%d" % b], ["ab%d" % b])
-            out = T[xn][:, b:1024:4]
-            if b < 3:
-                act(out, ab, 0.03125, ["ab%d" % b], ["%s_%d" % (xn, b)])
-            else:
-                ts(out, ab, 0.03125, OP.mult, ["ab%d" % b], ["%s_%d" % (xn, b)])
-        quant(xn, T[xn][:], ["%s_%d" % (xn, b) for b in range(4)])
+        zk = ["z%d_%d" % (t, b) for b in range(4)]
+        for hf in range(2):
+            quant("z%d" % t, z, zk, 128 * hf, 128 * hf + 128, "qz%d_%d" % (t, hf))
+            for b in range(4):
+                mm(4 * hf + b, "w", "z%d" % t, 128, ["qw", "qz%d_%d" % (t, hf)], col=128 * b, first=128 * hf)
+        for hf in range(2):
+            for b in range(4):
+                ab = T.ab[:, 512 * hf + b:512 * hf + 512:4]
+                tt(ab, T["pb%d" % (4 * hf + b)][:, 0:128], T.zz[:, 256 * b + 128 * hf:256 * b + 128 * hf + 128], OP.add,
+                   ["pb%d" % (4 * hf + b), "zz%d" % b], ["ab%d_%d" % (hf, b)])
+            if hf == 0:
+                act(T[xn][:, 0:512], T.ab[:, 0:512], 0.03125, ["ab0_%d" % b for b in range(4)], [xn + "_0"])
+        ts(T[xn][:, 512:1024], T.ab[:, 512:1024], 0.03125, OP.mult, ["ab1_%d" % b for b in range(4)], [xn + "_1"])
+        if not last:
+            scores_first(xn)
 
     q = "x%d" % ROUNDS
-    order("y", ["q" + q], [])
+    for hf in range(2):
+        quant(q, T[q], ["%s_%d" % (q, hf)], 128 * hf, 128 * hf + 128, "q%s_%d" % (q, hf))
+        mm(hf, "v", q, 128, ["qv", "q%s_%d" % (q, hf)], first=128 * hf)
+    order("y", ["q%s_0" % q, "q%s_1" % q], [])
     Y.dma_start(T.oc[:], T["q" + q][:].bitcast(dt.uint8)).then_inc(T.sem.dq, 16)
     for k in range(4):
         Y.dma_start(T.osc[4 * k:4 * k + 4, :], T["s" + q][32 * k:32 * k + 4, :]).then_inc(T.sem.dq, 16)
-    mm(T.ps[:, 0:128], "v", q, 128, [], ["ps"])
-    mm(T.ps2[:, 0:128], "v", q, 128, [], ["ps2"], first=128)
-    cp(T.ysb[:, 0:128], T.ps[:, 0:128], ["ps"], ["ysba"])
-    act(T.ysb[:, 128:256], T.ps2[:, 0:128], 1.0, ["ps2"], ["ysbb"])
-    order("y", ["ysba"], [])
-    Y.dma_start(T.y[:, 0:128], T.ysb[:, 0:128]).then_inc(T.sem.dq, 16)
-    order("s", ["ysbb"], [])
-    S.dma_start(T.y[:, 128:256], T.ysb[:, 128:256]).then_inc(T.sem.dy, 16)
+    act(T.ysb[:, 0:128], T.pb0[:, 0:128], 1.0, ["pb0"], ["ysba"])
+    cp(T.ysb[:, 128:256], T.pb1[:, 0:128], ["pb1"], ["ysbb"])
+    order("s", ["ysba"], [])
+    S.dma_start(T.y[:, 0:128], T.ysb[:, 0:128]).then_inc(T.sem.dy, 16)
+    order("y", ["ysbb"], [])
+    Y.dma_start(T.y[:, 128:256], T.ysb[:, 128:256]).then_inc(T.sem.dq, 16)
     for sem in ("vec", "sca", "ten", "gps", "loc"):
         wait("g", (sem, count[sem]))
-    for sem, val in (("dx", 16), ("du", 16), ("dp", 16), ("dr", 256), ("dw", 32), ("dv", 16), ("dq", 96), ("dy", 16), ("dl", 16)):
+    for sem, val in (("dx0", 16), ("dx1", 16), ("du", 16), ("dp", 16), ("dw", 32), ("dv", 16), ("dq", 96), ("dy", 16), ("dl", 16)):
         wait("g", (sem, val))
     for t in range(ROUNDS):
         wait("g", ("ca%d" % t, 2 * n_in))

@@ -6,19 +6,26 @@ ROUNDS = 3
 BIG = 1e29
 LIFT = 1024.0
 SINK = 2048.0
+WHOLE = 1.5 * 2.0 ** 23
 FIELD = sum(1 << b for b in (8, 9, 18, 19, 20))
-PAIR = 254 + 512
 
-CTILES = {"a": ("a", 0, 256, ["b", 15, 14, 13]), "b": ("b", 0, 192, [12, 11, 10, 9]), "d": ("b", 192, 64, [4, 3, 2, 1]), "c": ("c", 0, 128, [8, 7, 6, 5])}
-ON_SCALAR = [15, 12]
+CTILES = {"a": ("a", 0, ["b", 15, 14, 13]), "b": ("b", 0, [12, 11, 10, 9]), "d": ("b", 192, [4, 3, 2, 1]), "c": ("c", 0, [8, 7, 6, 5])}
+
+START = ("ee zd zc flat ik qzero ig flatb ktwo ones k zb za last pcol mid irs onesb offr offc eye lzero pickl gj kwa cfive vr qu qxx pick mask picks "
+         "offk kwb ctl rzero rlist")
+ROUND = ("a12 qx0 gg* a13 min0 xb11 ibf* xb12 xb13 qx1 scan0 qg* r6 r5 c6 min1 c5 r3 s7 scan1 r1 s4 k7 r2 s12 r14 k4 r10 r13 c1 r15 k12 blocks "
+         "r9 c2 c14 r11 c10 c15 r8 c3 qa qb bsum qc c9 c11 c8 qone c13 offl* whole* qtwo fthree* qe0* lzer ltwo ex cw* cy* rho qe3* put "
+         "mzone* mzzero* own* swapv qe1* mzstep* swaps wa* wb* ibn* hx0 hx1 hx2 hx3 xh get qe2* hd0 hd1 hd2 hd3 fy ss bits ok five ls qv* ol "
+         "mine vr theirs srch0 srch1 tsh0 tsh1 g00 g01 g02 g03 z00 z01 g10 qz0 z02 z03 g11 g12 z10 g13 z11 a00 qz1 z12 z13 xb00 a01 xb01 a02 "
+         "xb02 a03 xb03 a10 xb10 a11")
+TRACE = []
 
 PACKS = {
-    "rows": (256, "float32", ["irs", "ex", "yy", "fy", "sw", "vr", "lr"]),
-    "flist": (16, "float32", ["r16", "q1", "own", "lk", "i1k", "rs"]),
-    "ilist": (16, "int32", ["m16", "m16r", "ss", "tt"]),
-    "iwide": (32, "int32", ["pq", "pm"]),
-    "fwide": (32, "float32", ["mz", "md", "mo"]),
-    "cols": (1, "float32", ["k2", "e15", "offk"]),
+    "rows": (256, "float32", ["irs", "ex", "yy", "vr", "lr", "pw", "pv", "cy"]),
+    "flist": (16, "float32", ["r16", "q1", "rs"]),
+    "ilist": (16, "int32", ["ss", "tt"]),
+    "five": (80, "float32", ["mz", "mo"]),
+    "cols": (1, "float32", ["pcol", "k", "k2", "mid", "e15", "offk", "offr", "offc", "offl"]),
 }
 PLACE = {name: (buf, i * w, w) for buf, (w, _, names) in PACKS.items() for i, name in enumerate(names)}
 
@@ -45,30 +52,26 @@ def _scratch():
         sb("uint16", 16, "la%d" % t)
         sb("bfloat16", 1024, "z%d" % t)
         sb("bfloat16", 2048, "h%d" % t)
-    sb("bfloat16", 1024, "zz", "ab", "xh", "ca")
-    sb("bfloat16", 1280, "cb")
+    sb("bfloat16", 1024, "zz", "ab", "xh", "ca", "cb")
     mx(512, "w", "e")
     mx(128, "u", "r", "v", "g", "cc")
     mx(256, "ca")
     mx(320, "cb")
     sb("bfloat16", 520, "ee")
     sb("bfloat16", 512, "gj", "gg", "usb", "vsb", "cc")
-    sb("bfloat16", 128, "dif")
     sb("float32", 256, "fd1", "ffw", "ysb")
     sb("float32", 272, "kwa", "kwb", "ctl")
     sb("float32", 512, "irow")
-    sb("float32", 768, "pw")
+    sb("float32", 1328, "fy")
     sb("bfloat16", 768, "w")
     sb("bfloat16", 272, "t16")
-    sb("bfloat16", 256, "eqk", "fmsk", "d0r", "d0b", "ibf", "ibn", "bsum")
+    sb("bfloat16", 256, "fmsk", "d0r", "d0b", "ibf", "ibn", "bsum", "cw")
+    sb("float16", 256, "src")
     sb("int32", 16, "lst0")
     sb("bfloat16", 1920, "junk", "sgn")
     sb("int32", 1, "ipcol", "ik", "ig")
-    sb("float32", 1, "fkcol", "fg")
-    sb("int32", 8, "upick")
     sb("uint16", 8, "u16")
-    sb("uint16", 16, "ts16")
-    sb("uint16", 32, "pq16")
+    sb("uint16", 16, "ts16", "rho")
     for b in range(8):
         s["pb%d" % b] = ("psum", [128, 512], "float32")
     return s
@@ -111,12 +114,13 @@ def rank_program(g, core, T, topo):
             tok = writer[k]
             need[tok[0]] = max(need.get(tok[0], 0), tok[1])
         for k in writes:
-            for tok in ([] if chained or k not in writer else [writer[k]]) + [r for r in readers.get(k, []) if r[0] != own_sem.get(q)]:
+            for tok in ([] if chained or k not in writer else [writer[k]]) + readers.get(k, []):
                 need[tok[0]] = max(need.get(tok[0], 0), tok[1])
         for sem in need:
             wait(q, (sem, need[sem]))
 
     def note(tok, reads, writes):
+        TRACE.append((reads, writes))
         for k in reads:
             readers.setdefault(k, []).append(tok)
         for k in writes:
@@ -160,12 +164,15 @@ def rank_program(g, core, T, topo):
     def scan(out, d0, d1, reads, writes, init=0.0, op0=OP.mult, op1=OP.add):
         do("v", reads, writes, lambda: V.tensor_tensor_scan(out, d0, d1, init, op0, op1))
 
-    def quant(name, tile, reads, a=0, b=None, key=None):
+    def quant(name, tile, reads, a=0, b=None, keys=None):
         b = T["q" + name].shape[1] if b is None else b
-        do("v", reads, [key or "q" + name], lambda: V.quantize_mx(T["q" + name][:, a:b], T["s" + name][:, a:b], tile[:, 4 * a:4 * b]))
+        do("v", reads, keys or ["q" + name], lambda: V.quantize_mx(T["q" + name][:, a:b], T["s" + name][:, a:b], tile[:, 4 * a:4 * b]))
 
     def fillc(out, value, key):
         do("v", [], key, lambda: V.memset(out, value))
+
+    def fills(out, n, value, key):
+        act(out, T.irow[:, 0:n], 0.0, ["irow"], key, AF.Identity, value)
 
     def iota(out, pattern, cm, key, base=0):
         do("g", [], [key], lambda: g.iota(out, pattern, base, cm, allow_small_or_imprecise_dtypes=True))
@@ -174,251 +181,253 @@ def rank_program(g, core, T, topo):
         do("t", reads, ["pb%d" % bank],
            lambda: P.matmul_mx(T["pb%d" % bank][:, 0:k], T["q" + a][:, col:col + 128], T["s" + a][:, col:col + 128], T["q" + x][:, first:first + k], T["s" + x][:, first:first + k], start, stop), chained=not start)
 
-    load("y", "x0_0", T.x0[:, 0:512], T.x[:, 0:512], "dx0", 16)
+    def five(j):
+        return T.fy[:, 59 + 16 * j:1328:80]
+
     load("s", "usb", T.usb[:], T.u[:], "du", 16)
-    load("y", "x0_1", T.x0[:, 512:1024], T.x[:, 512:1024], "dx1", 16)
+    load("y", "x0_0", T.x0[:, 0:512], T.x[:, 0:512], "dx0", 16)
     load("y", "lst0", T.lst0[:], T.p[:], "dp", 16)
+    load("y", "x0_1", T.x0[:, 512:1024], T.x[:, 512:1024], "dx1", 16)
     load("y", "qw", T.qw[:].bitcast(dt.uint8), T.wc[:], "dw", 32)
     load("y", "qw", T.sw[:], T.ws[:], "dw", 32)
     load("y", "vsb", T.vsb[:], T.v[:], "dv", 16)
-
-    def lists(t):
-        ls = "ls%d" % t
-        cp(W("md", 1, 32, 2), T[ls][:], [ls], ["lf"])
-        ts(W("lk"), T[ls][:], 1024.0, OP.mult, [ls], ["lk"])
-        return lambda: tt(W("own"), W("i1k"), W("md", 1, 32, 2), OP.add, ["i1k", "lf"], ["own"])
-
-    def packed_row(t):
-        tt(W("vr"), T.irow[:].indirect(T["ls%d" % t][:]), W("irs"), OP.subtract, ["irow", "ls%d" % t, "irs"], ["vr"])
-
     iota(T.ipcol[:], [[1, 1]], 1, "ipcol")
-    iota(T.upick[:], [[16, 8]], 0, "upick")
-    iota(T.t16[:], [[0, 17], [1, 16]], 0, "t16")
-    iota(T.gj[:], [[1, 8], [0, 64]], 0, "gj")
-    iota(W("m16"), [[16, 16]], 0, "m16")
-    iota(W("m16r"), [[16, 16]], 0, "m16r", 15 - 256 - int(SINK))
-    iota(T.dif[:], [[1, 128]], -1, "dif")
     iota(T.irow[:], [[1, 512]], 0, "irow")
-    fillc(T.ca[:, 4 * 208:1024], 0.0, ["ca%d" % i for i in range(4)])
-    ts(T.ik[:], T.ipcol[:], 15, OP.bitwise_and, ["ipcol"], ["ik"])
-    ts(T.ig[:], T.ipcol[:], 4, OP.arith_shift_right, ["ipcol"], ["ig"])
-    fillc(T.cb[:, 4 * 144:1280], 0.0, ["cb%d" % i for i in range(4)] + ["cd%d" % i for i in range(4)])
-    cp(T.fkcol[:], T.ik[:], ["ik"], ["fkcol"])
-    ts(W("k2"), T.ik[:], 2.0, OP.add, ["ik"], ["k2"])
-    cp(T.u16[:], T.upick[:], ["upick"], ["u16"])
-    cp(T.fg[:], T.ig[:], ["ig"], ["fg"])
-    ts(W("e15"), T.fkcol[:], 15.0, OP.is_equal, ["fkcol"], ["e15"], LIFT, OP.mult)
-    fillc(T.cc[:, 4 * 80:512], 0.0, ["cc%d" % i for i in range(4)])
-    ts(T.eqk[:], T.t16[:, 0:256], T.fkcol[:, 0:1], OP.is_equal, ["t16", "fkcol"], ["eqk"], 1024.0, OP.mult)
-    ts(W("offk"), W("e15"), 256.0 - LIFT, OP.add, ["e15"], ["offk"])
-    quant("cb", T.cb, ["cb0"], 192, 320, "qcz")
-    fillc(W("rs", 0, 1), 0.0, ["rs0"])
-    fillc(W("mz"), 0.0, ["ok"])
-    fillc(T.ee[:], 0.0, ["ee"])
-    act(T.d0b[:], T.t16[:, 0:256], 1.0, ["t16"], ["d0b"], AF.Sign)
-    act(T.fmsk[:], T.eqk[:], 2 * BIG / 1024, ["eqk"], ["fmsk"], AF.Identity, -BIG)
-    act(T.d0r[:], T.d0b[:], 2 * BIG, ["d0b"], ["d0r"], AF.Identity, -BIG)
-    quant("u", T.usb, ["usb"])
-    do("v", ["qu", "u16"], ["qr"], lambda: V.tensor_copy(T.qr[:].bitcast(dt.uint32), T.qu[:].bitcast(dt.uint32).indirect(T.u16[:])))
-    do("s", ["qu", "u16"], ["qrs"], lambda: S.activation(T.sr[:], T.su[:].indirect(T.u16[:]), AF.Copy))
-    act(T.kwa[:], T.t16[:], -1.0, ["t16", "k2"], ["kwa"], AF.Relu, W("k2"))
-    act(T.kwb[:], T.kwa[:], 7 * LIFT, ["kwa"], ["kwb"], AF.Abs, -4 * LIFT)
+    iota(T.t16[:], [[0, 17], [1, 16]], 0, "t16")
 
+    slot_keys = {name: ["c%s%d" % (name, i) for i in range(4)] for name in CTILES}
+    slot_keys["a"] = ["blk0", "blk1"] + slot_keys["a"][1:]
     at = {m: 8 * m * (m - 1) for m in range(1, 16)}
     views = {}
-    for name, (buf, c0, k, slots) in CTILES.items():
+    for name, (buf, c0, slots) in CTILES.items():
         for i, m in enumerate(slots):
             if m != "b":
                 views[m] = (T["c" + buf][:, 4 * c0 + i:4 * c0 + 64 * m:4], "c%s%d" % (name, i))
-    slot_keys = {name: ["c%s%d" % (name, i) for i in range(4)] for name in CTILES}
     V0, VF, SF, PC = 0, 2, 3, 4
     UNPACK = [5, 6, 7, 1]
+    SCORES = [(V0, 0), (VF, 128)]
+    both = lambda name, b: ["%s0%d" % (name, b), "%s1%d" % (name, b)]
+    four = lambda name, hf: ["%s%d%d" % (name, hf, b) for b in range(4)]
+    half = lambda hf: slice(128 * hf, 128 * hf + 128)
+    wide = lambda hf: slice(512 * hf, 512 * hf + 512)
+    part = lambda hf, b: slice(512 * hf + b, 512 * hf + 512, 4)
+    score = lambda hf: T["pb%d" % SCORES[hf][0]][:, SCORES[hf][1]:SCORES[hf][1] + 128]
 
-    def latch(hf, bank, lo):
-        cols = slice(128 * hf, 128 * hf + 128)
-        first = lambda: tt(T.fd1[:, cols], T["pb%d" % bank][:, lo:lo + 128], T.fmsk[:, cols], OP.min, ["pb%d" % bank, "fmsk"], ["fd%d" % hf])
-        second = lambda: scan(T.ffw[:, cols], T.d0r[:, cols], T.fd1[:, cols], ["d0r", "fd%d" % hf], ["ffw%d" % hf], -BIG, OP.min, OP.max)
-        return first, second
+    def x_keys(t, hf):
+        return ["x0_%d" % hf] * 4 if t == 0 else four("x", hf)
 
-    def row(m):
+    def zeros(name):
+        buf, c0, slots = CTILES[name]
+        lo = 4 * (c0 + 16 * slots[3])
+        act(T["c" + buf][:, lo:lo + 192], T.ee[:, 0:192], 1.0, ["ee"], slot_keys[name][-4:])
+
+    def row(t, m):
         bank = V0 if m <= 8 else VF
         view, key = views[m]
         ts(view, T["pb%d" % bank][:, 0:16 * m], T.ffw[:, 16 * m + 15:16 * m + 16], OP.is_lt, ["pb%d" % bank, "ffw%d" % (m // 8)], [key])
 
-    def count_row(m):
+    def count_row(t, m):
         view, key = views[m]
-        if m in ON_SCALAR:
-            do("s", ["sgn%d" % m], [key, "rs%d" % m], lambda: S.activation(view, T.sgn[:, at[m]:at[m] + 16 * m], AF.Relu, accum_out=W("rs", m, m + 1)))
-        else:
-            do("s", [key], ["junk%d" % m, "rs%d" % m], lambda: S.activation(T.junk[:, at[m]:at[m] + 16 * m], view, AF.Copy, accum_out=W("rs", m, m + 1)))
+        do("s", [key], ["junk%d" % m, "rs%d" % m], lambda: S.activation(T.junk[:, at[m]:at[m] + 16 * m], view, AF.Copy, accum_out=W("rs", m, m + 1)))
 
-    def sign_row(m):
+    def sign_row(t, m):
         act(T.sgn[:, at[m]:at[m] + 16 * m], T["pb%d" % SF][:, 0:16 * m], -1.0, ["pb%d" % SF, "ffw%d" % (m // 8)], ["sgn%d" % m], AF.Sign, T.ffw[:, 16 * m + 15:16 * m + 16])
 
-    def scores_first(x):
-        quant(x, T[x], [x + "_0"], 0, 128, "q%s_0" % x)
-        mm(V0, "r", x, 128, ["qr", "qrs", "q%s_0" % x])
+    def keep_row(t, m):
+        view, key = views[m]
+        do("s", ["sgn%d" % m], [key, "rs%d" % m], lambda: S.activation(view, T.sgn[:, at[m]:at[m] + 16 * m], AF.Relu, accum_out=W("rs", m, m + 1)))
 
-    scores_first("x0")
-    for t in range(ROUNDS):
-        last = t == ROUNDS - 1
-        x, xn, ls, la = "x%d" % t, "x%d" % (t + 1), "ls%d" % (t + 1), "la%d" % t
-        h, z = T["h%d" % t], T["z%d" % t]
-        qx = ["q%s_0" % x, "q%s_1" % x]
-        min0, scan0 = latch(0, V0, 0)
-        min1, scan1 = latch(1, VF, 128)
-        quant(x, T[x], [x + "_1"], 128, 256, qx[1])
-        mm(VF, "r", x, 256, qx)
-        mm(SF, "r", x, 256, qx)
-        if t > 0:
-            lists(t)()
-            min0()
-        send(T["ql%d" % t][:].bitcast(dt.uint8), T["q" + x][:].bitcast(dt.uint8), "ca%d" % t, qx)
-        send(T["sl%d" % t][:], T["s" + x][:], "ca%d" % t, qx)
-        note(("ca%d" % t, 2 * n_in), [], ["ql%d" % t])
-        if t == 0:
-            ts(T.gg[:], T.gj[:], T.fg[:, 0:1], OP.is_equal, ["gj", "fg"], ["gg"])
-            min0()
-            quant("g", T.gg, ["gg"])
-            act(T.ctl[:], T.kwb[:], -1.0, ["kwb"], ["ctl"], AF.Identity, 4 * LIFT)
-        scan0()
-        if t == 0:
-            ts(W("r16"), W("m16r"), T.fkcol[:, 0:1], OP.subtract, ["m16r", "fkcol", "offk"], ["r16"], W("offk"), OP.add)
-            ts(W("i1k"), W("m16"), T.fkcol[:, 0:1], OP.add, ["m16", "fkcol"], ["i1k"], -1024.0, OP.mult)
-        for m in (7, 6, 5, 4):
-            row(m)
-        for m in (7, 6, 5):
-            count_row(m)
-        min1()
-        row(3)
-        row(2)
-        scan1()
-        row(1)
-        sign_row(15)
-        count_row(4)
-        count_row(15)
-        sign_row(12)
-        count_row(3)
-        count_row(12)
-        count_row(2)
-        count_row(1)
-        tt(T.ca[:, 0:1024:4], T["pb%d" % VF][:, 0:256], T.ffw[:], OP.is_le, ["pb%d" % VF, "ffw0", "ffw1"], ["ca0"])
-        for m in (14, 13, 11):
-            row(m)
-            count_row(m)
+    def sum_a(t):
         quant("ca", T.ca, slot_keys["a"])
         mm(PC, "g", "ca", 256, ["qg", "qca"], True, False)
-        for m in (10, 9, 8):
-            row(m)
-            count_row(m)
-        quant("cb", T.cb, slot_keys["b"] + slot_keys["d"] + ["qcz"], 0, 256)
+
+    def sum_b(t):
+        quant("cb", T.cb, slot_keys["b"] + slot_keys["d"], 0, 256)
         mm(PC, "g", "cb", 192, ["qcb"], False, False)
         mm(PC, "g", "cb", 128, ["qcb"], False, False, first=192)
+
+    def sum_c(t):
         quant("cc", T.cc, slot_keys["c"])
         mm(PC, "g", "cc", 128, ["qcc"], False, True)
-        scan(T.bsum[:], T.d0b[:], T.ca[:, 0:1024:4], ["d0b", "ca0"], ["bsum"])
-        if t == 0:
-            cp(T.ls0[:], T.lst0[:], ["lst0"], ["ls0"])
-            act(W("irs"), T.irow[:, 0:256], 1.0 / 1024.0, ["irow"], ["irs"])
-            act(T.pw[:, 0:512], T.irow[:], 1.0, ["irow"], ["pw"])
-            act(T.pw[:, 512:768], T.irow[:, 0:256], 1.0, ["irow"], ["pw"])
-        tt(W("q1"), W("r16"), T.bsum[:, 15:256:16], OP.subtract, ["r16", "bsum"], ["q1"])
-        if t == 0:
-            ts(T.ee[:, 4:516:4], T.dif[:], 0.0, OP.is_equal, ["dif"], ["ee"])
-        tt(T.ctl[:, 16:272:16], W("q1"), W("rs"), OP.subtract, ["q1"] + ["rs%d" % m for m in range(16)], ["ctl"])
-        if t == 0:
-            own0 = lists(0)
-        scan(W("ex"), T["pb%d" % PC][:, 0:256], T.ctl[:, 1:257], ["ctl", "pb%d" % PC], ["ex"], 0.0, OP.max, OP.add)
 
-        def unpacker(b):
-            if t == 0:
-                do("v", ["ee"], ["qe%d" % b], lambda: V.quantize_mx(T.qe[:, 128 * b:128 * b + 128], T.se[:, 128 * b:128 * b + 128], T.ee[:, 4 - b:516 - b]))
-        if t == 0:
-            packed_row(0)
-        ex = W("ex", 15, 256, 16)
-        ts(W("pq", 0, 16), ex, SINK, OP.add, ["ex"], ["pqa"], 513.0, OP.mult)
-        ts(W("pq", 16, 32), ex, 513.0, OP.mult, ["ex"], ["pqb"], 513.0 * SINK + 512.0, OP.add)
-        if t == 0:
-            own0()
-        ts(W("pm"), W("pq"), PAIR, OP.bitwise_and, ["pqa", "pqb"], ["pm"])
-        unpacker(0)
-        cp(T.pq16[:], W("pm"), ["pm"], ["pq16"])
-        unpacker(1)
-        cp(T.pw[:].indirect(T.pq16[:, 0:16]), W("vr"), ["pq16", "vr"], ["pw"])
-        unpacker(2)
-        tt(W("yy"), T.pw[:].indirect(T.pq16[:, 16:32]), T.eqk[:], OP.mult, ["pw", "pq16", "eqk"], ["yy"])
-        unpacker(3)
-        if t == 0:
-            act(T.ibf[:], T.irow[:, 0:256], 1.0, ["irow"], ["ibf"])
-            act(T.ibn[:], T.irow[:, 0:256], 1.0, ["irow"], ["ibn"], AF.Identity, -256.0)
-            act(T.w[:, 0:512], T.irow[:], 0.0, ["irow"], ["w"])
-            act(T.w[:, 512:768], T.irow[:, 0:256], 0.0, ["irow"], ["w"])
-        for b in range(4):
-            act(h[:, 512 * b + 256:512 * b + 512], T[x][:, b:1024:4], 0.5, [x + "_0", x + "_1"], ["hx%d_%d" % (t, b)])
-        act(T.xh[:], T[x][:], 0.5, [x + "_0", x + "_1"], ["xh"])
-        for b in range(4):
-            mm(UNPACK[b], "e", "l%d" % t, 256, ["qe%d" % b, "ql%d" % t], col=128 * b)
-            act(h[:, 512 * b:512 * b + 256], T["pb%d" % UNPACK[b]][:, 0:256], 0.5, ["pb%d" % UNPACK[b]], ["hd%d_%d" % (t, b)])
-        scan(W("fy"), T.d0b[:], W("yy"), ["d0b", "yy"], ["fy"])
-        fy = W("fy", 15, 256, 16)
-        tt(W("ss"), fy, W("own"), OP.add, ["fy", "own"], ["ss"])
-        tt(W("md", 0, 32, 2), fy, W("lk"), OP.subtract, ["fy", "lk"], ["y"])
-        ts(W("tt"), W("ss"), FIELD, OP.bitwise_and, ["ss"], ["tt"])
-        ts(W("mz", 1, 32, 2), W("tt"), 0.0, OP.is_equal, ["tt"], ["ok"], 1.0 / 1024.0, OP.mult)
-        scan(W("mo"), W("mz"), W("md"), ["ok", "y", "lf"], ["mo"])
-        ts(T[ls][:], W("mo", 1, 32, 2), 0.25, OP.add, ["mo"], [ls])
-        send(T[la][:], T[ls][:], la, [ls])
-        note((la, n_in), [], [la])
-        cp(T.w[:, 256:768].indirect(T[ls][:]), T.ibf[:], [ls, "ibf"], ["w"])
-        if last:
-            act(W("lr"), T.irow[:].indirect(T[ls][:]), 1.0, ["irow", ls], ["lr"])
+    def quant_state(t, hf):
+        x = "x%d" % t
+        quant(x, T[x], x_keys(t, hf), 128 * hf, 128 * hf + 128, ["qx%d" % hf])
+        if t == ROUNDS:
+            mm(hf, "v", x, 128, ["qv", "qx%d" % hf], first=128 * hf)
+        elif hf == 1:
+            mm(VF, "r", x, 256, ["qx0", "qx1"])
+            mm(SF, "r", x, 256, ["qx0", "qx1"])
+            send(T["ql%d" % t][:].bitcast(dt.uint8), T["q" + x][:].bitcast(dt.uint8), "ca%d" % t, ["qx0", "qx1"])
+            send(T["sl%d" % t][:], T["s" + x][:], "ca%d" % t, ["qx0", "qx1"])
+            note(("ca%d" % t, 2 * n_in), [], ["ql"])
+        elif t > 0:
+            mm(V0, "r", x, 128, ["qr", "qrs", "qx0"])
+
+    def pick_scales(t):
+        do("s", ["qu", "u16"], ["qrs"], lambda: S.activation(T.sr[:], T.su[:].indirect(T.u16[:]), AF.Copy))
+        mm(V0, "r", "x0", 128, ["qr", "qrs", "qx0"])
+
+    def landings(t):
+        ls, la = "ls%d" % (t + 1), "la%d" % t
+        ts(T[ls][:], W("mo", 3, 80, 5), -WHOLE, OP.add, ["mo"], ["ls"])
+        send(T[la][:], T[ls][:], la, ["ls"])
+        note((la, n_in), [], ["la"])
+
+    def packed_row(t, a=0, b=4):
+        if t < ROUNDS:
+            tt(W("vr", 64 * a, 64 * b), T.irow[:].indirect(T["ls%d" % t][:, 4 * a:4 * b]), W("irs", 64 * a, 64 * b), OP.subtract, ["irow", "ls", "irs"], ["vr%d" % i for i in range(a, b)])
+
+    def store_landings(t):
+        if t == ROUNDS - 1:
+            act(W("lr"), T.irow[:].indirect(T["ls%d" % ROUNDS][:]), 1.0, ["irow", "ls"], ["lr"])
             order("y", ["lr"], [])
             lo = PLACE["lr"][1]
             Y.dma_start(T.ol[:], T.rows[0:128:16, lo:lo + 256]).then_inc(T.sem.dl, 16)
-        else:
-            packed_row(t + 1)
-        if t == 0:
-            quant("v", T.vsb, ["vsb"])
-        cp(T.w[:, 0:512].indirect(T[la][:]), T.ibn[:], [la, "ibn"], ["w"])
-        scan(W("sw"), T.ctl[:, 0:256], T.w[:, 256:512], ["ctl", "w"], ["sw"], 0.0, OP.add, OP.max)
-        ts(T.ts16[:], W("sw", 15, 256, 16), W("offk"), OP.add, ["sw", "offk"], ["ts16"])
+
+    def unpack(t, b):
+        mm(UNPACK[b], "e", "l%d" % t, 256, ["qe%d" % b, "ql"], col=128 * b)
+        act(T["h%d" % t][:, 512 * b:512 * b + 256], T["pb%d" % UNPACK[b]][:, 0:256], 0.5, ["pb%d" % UNPACK[b]], ["hd%d" % b])
+
+    def catch(t, cols, offsets, b, keys):
+        tt(T["z%d" % t][:, cols], T["h%d" % t][:, 512 * b:512 * b + 512].indirect(offsets), T.xh[:, cols], OP.add, ["ts" + k[1] for k in keys] + ["xh", "hx%d" % b, "hd%d" % b], keys)
+
+    def layer(t, hf):
+        z = "z%d" % t
+        quant(z, T[z], four("z", hf), 128 * hf, 128 * hf + 128, ["qz%d" % hf])
         for b in range(4):
-            tt(z[:, b:1024:4], h[:, 512 * b:512 * b + 512].indirect(T.ts16[:]), T.xh[:, b:1024:4], OP.add,
-               ["ts16", "xh", "hx%d_%d" % (t, b), "hd%d_%d" % (t, b)], ["z%d_%d" % (t, b)])
-            act(T.zz[:, 256 * b:256 * b + 256], z[:, b:1024:4], 32.0, ["z%d_%d" % (t, b)], ["zz%d" % b])
-        zk = ["z%d_%d" % (t, b) for b in range(4)]
-        for hf in range(2):
-            quant("z%d" % t, z, zk, 128 * hf, 128 * hf + 128, "qz%d_%d" % (t, hf))
-            for b in range(4):
-                mm(4 * hf + b, "w", "z%d" % t, 128, ["qw", "qz%d_%d" % (t, hf)], col=128 * b, first=128 * hf)
-        for hf in range(2):
-            for b in range(4):
-                ab = T.ab[:, 512 * hf + b:512 * hf + 512:4]
-                tt(ab, T["pb%d" % (4 * hf + b)][:, 0:128], T.zz[:, 256 * b + 128 * hf:256 * b + 128 * hf + 128], OP.add,
-                   ["pb%d" % (4 * hf + b), "zz%d" % b], ["ab%d_%d" % (hf, b)])
-            if hf == 0:
-                act(T[xn][:, 0:512], T.ab[:, 0:512], 0.03125, ["ab0_%d" % b for b in range(4)], [xn + "_0"])
-        ts(T[xn][:, 512:1024], T.ab[:, 512:1024], 0.03125, OP.mult, ["ab1_%d" % b for b in range(4)], [xn + "_1"])
-        if not last:
-            scores_first(xn)
+            mm(4 * hf + b, "w", z, 128, ["qw", "qz%d" % hf], col=128 * b, first=128 * hf)
+
+    STEP = {
+        "ee": lambda t: fillc(T.ee[:], 0.0, ["ee"]),
+        "za": lambda t: zeros("a"), "zb": lambda t: zeros("b"), "zc": lambda t: zeros("c"), "zd": lambda t: zeros("d"),
+        "ones": lambda t: fillc(T.d0b[:], 1.0, ["d0b"]), "onesb": lambda t: fillc(T.d0b[:, 0:256:16], 0.0, ["d0b"]),
+        "flat": lambda t: fillc(T.d0r[:], 0.0, ["d0r"]), "flatb": lambda t: fillc(T.d0r[:, 0:256:16], -2 * BIG, ["d0r"]),
+        "ik": lambda t: ts(T.ik[:], T.ipcol[:], 15, OP.bitwise_and, ["ipcol"], ["ik"]),
+        "ig": lambda t: ts(T.ig[:], T.ipcol[:], 4, OP.arith_shift_right, ["ipcol"], ["ig"]),
+        "pcol": lambda t: cp(W("pcol"), T.ipcol[:], ["ipcol"], ["pcol"]),
+        "qzero": lambda t: do("v", ["ee"], ["qcb"], lambda: V.quantize_mx(T.qcb[:, 192:320], T.scb[:, 192:320], T.ee[:, 0:512])),
+        "k": lambda t, m=None: cp(W("k"), T.ik[:], ["ik"], ["k"]) if m is None else keep_row(t, m),
+        "ktwo": lambda t: ts(W("k2"), T.ik[:], 2.0, OP.add, ["ik"], ["k2"]),
+        "mid": lambda t: ts(W("mid"), T.ig[:], -64.0, OP.mult, ["ig"], ["mid"], -31.5, OP.add),
+        "last": lambda t: ts(W("e15"), T.ik[:], 15.0, OP.is_equal, ["ik"], ["e15"], LIFT, OP.mult),
+        "pickl": lambda t: cp(T.u16[:], T.irow[:, 0:128:16], ["irow"], ["u16"]),
+        "eye": lambda t: ts(T.ee[:, 4:516:4], T.irow[:, 0:128], W("pcol"), OP.is_equal, ["irow", "pcol"], ["ee"]),
+        "irs": lambda t: act(W("irs"), T.irow[:, 0:256], 1.0 / 1024.0, ["irow"], ["irs"]),
+        "gj": lambda t: act(T.gj[:], T.irow[:], 1.0, ["irow", "mid"], ["gj"], AF.Abs, W("mid")),
+        "offr": lambda t: ts(W("offr"), W("e15"), W("k"), OP.subtract, ["e15", "k"], ["offr"], 15.0 - LIFT - SINK, OP.add),
+        "offc": lambda t: ts(W("offc"), W("k"), W("e15"), OP.subtract, ["e15", "k"], ["offc"], LIFT + WHOLE / 1024, OP.add),
+        "lzero": lambda t: cp(T.ls0[:], T.lst0[:], ["lst0"], ["ls"]),
+        "cfive": lambda t: ts(five(4), T.irow[:, 0:256:16], W("offc"), OP.add, ["irow", "offc"], ["five4"], -1024.0, OP.mult),
+        "kwa": lambda t: act(T.kwa[:], T.t16[:], -1.0, ["t16", "k2"], ["kwa"], AF.Relu, W("k2")),
+        "kwb": lambda t: act(T.kwb[:], T.kwa[:], 7 * LIFT, ["kwa"], ["kwb"], AF.Abs, -4 * LIFT),
+        "ctl": lambda t: act(T.ctl[:], T.kwb[:], -1.0, ["kwb"], ["ctl"], AF.Identity, 4 * LIFT),
+        "cw": lambda t: act(T.cw[:], T.kwb[:, 0:256], -1.0, ["kwb"], ["cw"], AF.Identity, 4 * LIFT),
+        "cy": lambda t: act(W("cy"), T.kwb[:, 0:256], -1024.0, ["kwb"], ["cy"], AF.Identity, 4096 * LIFT),
+        "mask": lambda t: ts(T.fmsk[:], T.t16[:, 0:256], W("k"), OP.not_equal, ["t16", "k"], ["fmsk"], -BIG, OP.mult),
+        "rlist": lambda t: act(W("r16"), T.irow[:, 0:256:16], 1.0, ["irow", "offr"], ["r16"], AF.Identity, W("offr")),
+        "rzero": lambda t: fills(W("rs", 0, 1), 1, 0.0, ["rs0"]),
+        "qu": lambda t: quant("u", T.usb, ["usb"]), "qv": lambda t: quant("v", T.vsb, ["vsb"]), "qxx": lambda t: quant_state(0, 0),
+        "pick": lambda t: do("v", ["qu", "u16"], ["qr"], lambda: V.tensor_copy(T.qr[:].bitcast(dt.uint32), T.qu[:].bitcast(dt.uint32).indirect(T.u16[:]))),
+        "picks": pick_scales,
+        "gg": lambda t: ts(T.gg[:], T.gj[:], 32.0, OP.is_lt, ["gj"], ["gg"]),
+        "qg": lambda t: quant("g", T.gg, ["gg"]),
+        "qe": lambda t, b: do("v", ["ee"], ["qe%d" % b], lambda: V.quantize_mx(T.qe[:, 128 * b:128 * b + 128], T.se[:, 128 * b:128 * b + 128], T.ee[:, 4 - b:516 - b])),
+        "whole": lambda t: ts(W("mo", 3, 80, 5), T.lst0[:], WHOLE, OP.add, ["lst0"], ["mo"]),
+        "own": lambda t: tt(W("mo", 4, 80, 5), W("mo", 3, 80, 5), five(4), OP.add, ["mo", "five4"], ["own"]),
+        "offl": lambda t: act(W("offl"), W("e15"), -1.0, ["e15"], ["offl"], AF.Identity, LIFT - WHOLE),
+        "offk": lambda t: act(W("offk"), W("e15"), 1.0, ["e15"], ["offk"], AF.Identity, 256.0 - LIFT),
+        "fthree": lambda t: fills(five(3), 16, WHOLE, ["five3"]),
+        "mzone": lambda t: fills(W("mz"), 80, 1.0, ["mz"]),
+        "mzzero": lambda t: fills(W("mz", 0, 80, 5), 16, 0.0, ["mz"]),
+        "mzstep": lambda t: fills(W("mz", 1, 80, 5), 16, -1024.0, ["mz"]),
+        "ibf": lambda t: act(T.ibf[:], T.irow[:, 0:256], 1.0, ["irow"], ["ibf"]),
+        "ibn": lambda t: act(T.ibn[:], T.irow[:, 0:256], 1.0, ["irow"], ["ibn"], AF.Identity, -256.0),
+        "wa": lambda t: fills(T.w[:, 0:512], 512, 0.0, ["w"]), "wb": lambda t: fills(T.w[:, 512:768], 256, 0.0, ["w"]),
+        "qx": quant_state,
+        "min": lambda t, hf: tt(T.fd1[:, half(hf)], score(hf), T.fmsk[:, half(hf)], OP.add, ["pb%d" % SCORES[hf][0], "fmsk"], ["fd%d" % hf]),
+        "scan": lambda t, hf: scan(T.ffw[:, half(hf)], T.d0r[:, half(hf)], T.fd1[:, half(hf)], ["d0r", "fd%d" % hf], ["ffw%d" % hf], -BIG, OP.add, OP.max),
+        "blocks": lambda t: tt(T.ca[:, 0:1024:4], T["pb%d" % VF][:, 0:256], T.ffw[:], OP.is_le, ["pb%d" % VF, "ffw0", "ffw1"], ["blk0", "blk1"]),
+        "blk": lambda t, hf: tt(T.ca[:, part(hf, 0)], score(hf), T.ffw[:, half(hf)], OP.is_le, ["pb%d" % SCORES[hf][0], "ffw%d" % hf], ["blk%d" % hf]),
+        "r": row, "c": count_row, "s": sign_row, "qa": sum_a, "qb": sum_b, "qc": sum_c,
+        "bsum": lambda t: scan(T.bsum[:], T.d0b[:], T.ca[:, 0:1024:4], ["d0b", "blk0", "blk1"], ["bsum"]),
+        "qone": lambda t: tt(W("q1"), W("r16"), T.bsum[:, 15:256:16], OP.subtract, ["r16", "bsum"], ["q1"]),
+        "qtwo": lambda t: tt(T.ctl[:, 16:272:16], W("q1"), W("rs"), OP.subtract, ["q1"] + ["rs%d" % m for m in range(16)], ["ctl"]),
+        "ex": lambda t: scan(W("ex"), T["pb%d" % PC][:, 0:256], T.ctl[:, 1:257], ["ctl", "pb%d" % PC], ["ex"], 0.0, OP.max, OP.add),
+        "rho": lambda t: ts(T.rho[:], W("ex", 15, 256, 16), SINK, OP.add, ["ex"], ["rho"]),
+        "lzer": lambda t: act(five(0), W("mo", 3, 80, 5), 1.0, ["mo", "offl"], ["five0"], AF.Identity, W("offl")),
+        "ltwo": lambda t: act(five(2), W("mo", 3, 80, 5), 1.0, ["mo"], ["five2"], AF.Identity, -WHOLE),
+        "put": lambda t: cp(W("pw").indirect(T.rho[:]), W("vr"), ["rho", "vr0", "vr1", "vr2", "vr3"], ["pw"]),
+        "swaps": lambda t: act(W("pv", 0, 256, 2), W("pw", 1, 256, 2), 1.0, ["pw"], ["pve"]),
+        "swapw": lambda t: cp(W("pv", 0, 256, 2), W("pw", 1, 256, 2), ["pw"], ["pve"]),
+        "swapv": lambda t: cp(W("pv", 1, 256, 2), W("pw", 0, 256, 2), ["pw"], ["pvo"]),
+        "get": lambda t: ts(W("yy"), W("pv").indirect(T.rho[:]), 1024.0, OP.mult, ["pve", "pvo", "rho"], ["yy0", "yy1"]),
+        "fy": lambda t: scan(T.fy[:, 0:1280:5], W("cy"), W("yy"), ["cy", "yy0", "yy1"], ["five10", "five11"], 0.0, OP.add, OP.max),
+        "ss": lambda t: tt(W("ss"), five(1), W("mo", 4, 80, 5), OP.add, ["five10", "five11", "own"], ["ss"]),
+        "bits": lambda t: ts(W("tt"), W("ss"), FIELD, OP.bitwise_and, ["ss"], ["tt"]),
+        "ok": lambda t: ts(W("mz", 2, 80, 5), W("tt"), 0.0, OP.is_equal, ["tt"], ["mz"], 1.0 / 1024.0, OP.mult),
+        "five": lambda t: scan(W("mo"), W("mz"), T.fy[:, 59:1328:16], ["mz", "five0", "five10", "five11", "five2", "five3", "five4"], ["mo", "own"]),
+        "geth": lambda t, hf: ts(W("yy", 128 * hf, 128 * hf + 128), W("pv").indirect(T.rho[:, 8 * hf:8 * hf + 8]), 1024.0, OP.mult, ["pve", "pvo", "rho"], ["yy%d" % hf]),
+        "fyh": lambda t, hf: scan(T.fy[:, 640 * hf:640 * hf + 640:5], W("cy", 128 * hf, 128 * hf + 128), W("yy", 128 * hf, 128 * hf + 128), ["cy", "yy%d" % hf], ["five1%d" % hf], 0.0, OP.add, OP.max),
+        "ls": landings, "ol": store_landings,
+        "vr": lambda t, a=0, b=4: packed_row(t + 1, a, b),
+        "mine": lambda t: cp(T.w[:, 256:768].indirect(T["ls%d" % (t + 1)][:]), T.ibf[:], ["ls", "ibf"], ["w"]),
+        "theirs": lambda t: cp(T.w[:, 0:512].indirect(T["la%d" % t][:]), T.ibn[:], ["la", "ibn"], ["w"]),
+        "src": lambda t: scan(T.src[:], T.cw[:], T.w[:, 256:512], ["cw", "w"], ["src0", "src1"], 0.0, OP.add, OP.max),
+        "ts": lambda t: ts(T.ts16[:], T.src[:, 15:256:16], W("offk"), OP.add, ["src0", "src1", "offk"], ["ts0", "ts1"]),
+        "srch": lambda t, hf: scan(T.src[:, half(hf)], T.cw[:, half(hf)], T.w[:, 256 + 128 * hf:384 + 128 * hf], ["cw", "w"], ["src%d" % hf], 0.0, OP.add, OP.max),
+        "tsh": lambda t, hf: ts(T.ts16[:, 8 * hf:8 * hf + 8], T.src[:, 128 * hf + 15:128 * hf + 128:16], W("offk"), OP.add, ["src%d" % hf, "offk"], ["ts%d" % hf]),
+        "hx": lambda t, b: act(T["h%d" % t][:, 512 * b + 256:512 * b + 512], T["x%d" % t][:, b:1024:4], 0.5, x_keys(t, 0) + x_keys(t, 1), ["hx%d" % b]),
+        "xh": lambda t: act(T.xh[:], T["x%d" % t][:], 0.5, x_keys(t, 0) + x_keys(t, 1), ["xh"]),
+        "hd": unpack,
+        "G": lambda t, b: catch(t, slice(b, 1024, 4), T.ts16[:], b, both("z", b)),
+        "g": lambda t, hf, b: catch(t, part(hf, b), T.ts16[:, 8 * hf:8 * hf + 8], b, ["z%d%d" % (hf, b)]),
+        "Z": lambda t, b: act(T.zz[:, b:1024:4], T["z%d" % t][:, b:1024:4], 32.0, both("z", b), both("zz", b)),
+        "z": lambda t, hf, b: act(T.zz[:, part(hf, b)], T["z%d" % t][:, part(hf, b)], 32.0, ["z%d%d" % (hf, b)], ["zz%d%d" % (hf, b)]),
+        "qz": layer,
+        "a": lambda t, hf, b: tt(T.ab[:, part(hf, b)], T["pb%d" % (4 * hf + b)][:, 0:128], T.zz[:, part(hf, b)], OP.add, ["pb%d" % (4 * hf + b), "zz%d%d" % (hf, b)], ["ab%d%d" % (hf, b)]),
+        "xv": lambda t, hf: ts(T["x%d" % (t + 1)][:, wide(hf)], T.ab[:, wide(hf)], 0.03125, OP.mult, four("ab", hf), four("x", hf)),
+        "xs": lambda t, hf: act(T["x%d" % (t + 1)][:, wide(hf)], T.ab[:, wide(hf)], 0.03125, four("ab", hf), four("x", hf)),
+        "xb": lambda t, hf, b: act(T["x%d" % (t + 1)][:, part(hf, b)], T.ab[:, part(hf, b)], 0.03125, ["ab%d%d" % (hf, b)], ["x%d%d" % (hf, b)]),
+    }
+    STATE = ("a", "xv", "xs", "xb", "z", "Z", "g", "qz", "vr")
+
+    def step(word, t):
+        name = word.rstrip("0123456789")
+        digits = word[len(name):]
+        TRACE.append(word)
+        STEP[name](t, *([int(digits)] if digits and name in "rcsk" else [int(d) for d in digits]))
+
+    for word in START.split():
+        step(word, -1)
+    words = ROUND.split()
+    front = words.index("ls")
+    for t in range(ROUNDS + 1):
+        for i, word in enumerate(words):
+            name = word.rstrip("0123456789*")
+            if word.endswith("*") and t > 0:
+                continue
+            if name in STATE or word == "qx0":
+                late = i < front
+                if late and t > 0 or not late and t < ROUNDS:
+                    step(word, t - late + (word == "qx0"))
+            elif t < ROUNDS or word == "qx1":
+                step(word.rstrip("*"), t)
 
     q = "x%d" % ROUNDS
-    for hf in range(2):
-        quant(q, T[q], ["%s_%d" % (q, hf)], 128 * hf, 128 * hf + 128, "q%s_%d" % (q, hf))
-        mm(hf, "v", q, 128, ["qv", "q%s_%d" % (q, hf)], first=128 * hf)
-    order("y", ["q%s_0" % q, "q%s_1" % q], [])
+    act(T.ysb[:, 0:128], T.pb0[:, 0:128], 1.0, ["pb0"], ["ysb0"])
+    order("s", ["ysb0"], [])
+    S.dma_start(T.y[:, 0:128], T.ysb[:, 0:128]).then_inc(T.sem.dy, 16)
+    order("y", ["qx0", "qx1"], [])
     Y.dma_start(T.oc[:], T["q" + q][:].bitcast(dt.uint8)).then_inc(T.sem.dq, 16)
     for k in range(4):
         Y.dma_start(T.osc[4 * k:4 * k + 4, :], T["s" + q][32 * k:32 * k + 4, :]).then_inc(T.sem.dq, 16)
-    act(T.ysb[:, 0:128], T.pb0[:, 0:128], 1.0, ["pb0"], ["ysba"])
-    cp(T.ysb[:, 128:256], T.pb1[:, 0:128], ["pb1"], ["ysbb"])
-    order("s", ["ysba"], [])
-    S.dma_start(T.y[:, 0:128], T.ysb[:, 0:128]).then_inc(T.sem.dy, 16)
-    order("y", ["ysbb"], [])
-    Y.dma_start(T.y[:, 128:256], T.ysb[:, 128:256]).then_inc(T.sem.dq, 16)
+    act(T.ysb[:, 128:256], T.pb1[:, 0:128], 1.0, ["pb1"], ["ysb1"])
+    order("s", ["ysb1"], [])
+    S.dma_start(T.y[:, 128:256], T.ysb[:, 128:256]).then_inc(T.sem.dy, 16)
     for sem in ("vec", "sca", "ten", "gps", "loc"):
         wait("g", (sem, count[sem]))
-    for sem, val in (("dx0", 16), ("dx1", 16), ("du", 16), ("dp", 16), ("dw", 32), ("dv", 16), ("dq", 96), ("dy", 16), ("dl", 16)):
+    for sem, val in (("dx0", 16), ("dx1", 16), ("du", 16), ("dp", 16), ("dw", 32), ("dv", 16), ("dq", 80), ("dy", 32), ("dl", 16)):
         wait("g", (sem, val))
     for t in range(ROUNDS):
         wait("g", ("ca%d" % t, 2 * n_in))

from concourse.mybir import dt, AluOpType, ActivationFunctionType

OP = AluOpType
AF = ActivationFunctionType
ROUNDS = 3
BIG = 1e29
LIFT = 1024.0
SINK = 2048.0
WHOLE = 1.5 * 2.0 ** 23
FIELD = sum(1 << b for b in (8, 9, 18, 19, 20))

CTILES = {"a": ("a", 0, ["b", 15, 14, 13]), "b": ("b", 0, [12, 11, 10, 9]), "d": ("b", 192, [4, 3, 2, 1]), "c": ("c", 0, [8, 7, 6, 5])}

START = ("ee zd zc flat ik qzero ig flatb ktwo ones k zb za last pcol mid irs onesb offr offc eye lzero pickl gj kwa cfive vr qu qxx pick mask picks "
         "offk kwb ctl rzero rlist")
ROUND = ("a12 qx0 gg* a13 min0 xb11 ibf* xb12 xb13 qx1 scan0 qg* r6 r5 c6 min1 c5 r3 s7 scan1 r1 s4 k7 r2 s12 r14 k4 r10 r13 c1 r15 k12 blocks "
         "r9 c2 c14 r11 c10 c15 r8 c3 qa qb bsum qc c9 c11 c8 qone c13 offl* whole* qtwo fthree* qe0* lzer ltwo ex cw* cy* rho qe3* put "
         "mzone* mzzero* own* swapv qe1* mzstep* swaps wa* wb* ibn* hx0 hx1 hx2 hx3 xh get qe2* hd0 hd1 hd2 hd3 fy ss bits ok five ls qv* ol "
         "mine vr theirs srch0 srch1 tsh0 tsh1 g00 g01 g02 g03 z00 z01 g10 qz0 z02 z03 g11 g12 z10 g13 z11 a00 qz1 z12 z13 xb00 a01 xb01 a02 "
         "xb02 a03 xb03 a10 xb10 a11")
TRACE = []

PACKS = {
    "rows": (256, "float32", ["irs", "ex", "yy", "vr", "lr", "pw", "pv", "cy"]),
    "flist": (16, "float32", ["r16", "q1", "rs"]),
    "ilist": (16, "int32", ["ss", "tt"]),
    "five": (80, "float32", ["mz", "mo"]),
    "cols": (1, "float32", ["pcol", "k", "k2", "mid", "e15", "offk", "offr", "offc", "offl"]),
}
PLACE = {name: (buf, i * w, w) for buf, (w, _, names) in PACKS.items() for i, name in enumerate(names)}


def _scratch():
    s = {}

    def sb(d, n, *names):
        for name in names:
            s[name] = ("sbuf", [128, n], d)

    def mx(n, *names):
        for name in names:
            sb("float8_e4m3fn_x4", n, "q" + name)
            sb("uint8", n, "s" + name)
    for buf, (w, d, names) in PACKS.items():
        sb(d, w * len(names), buf)
    for t in range(ROUNDS + 1):
        sb("bfloat16", 1024, "x%d" % t)
        mx(256, "x%d" % t)
        sb("uint16", 16, "ls%d" % t)
    for t in range(ROUNDS):
        mx(256, "l%d" % t, "z%d" % t)
        sb("uint16", 16, "la%d" % t)
        sb("bfloat16", 1024, "z%d" % t)
        sb("bfloat16", 2048, "h%d" % t)
    sb("bfloat16", 1024, "zz", "ab", "xh", "ca", "cb")
    mx(512, "w", "e")
    mx(128, "u", "r", "v", "g", "cc")
    mx(256, "ca")
    mx(320, "cb")
    sb("bfloat16", 520, "ee")
    sb("bfloat16", 512, "gj", "gg", "usb", "vsb", "cc")
    sb("float32", 256, "fd1", "ffw", "ysb")
    sb("float32", 272, "kwa", "kwb", "ctl")
    sb("float32", 512, "irow")
    sb("float32", 1328, "fy")
    sb("bfloat16", 768, "w")
    sb("bfloat16", 272, "t16")
    sb("bfloat16", 256, "fmsk", "d0r", "d0b", "ibf", "ibn", "bsum", "cw")
    sb("float16", 256, "src")
    sb("int32", 16, "lst0")
    sb("bfloat16", 1920, "junk", "sgn")
    sb("int32", 1, "ipcol", "ik", "ig")
    sb("uint16", 8, "u16")
    sb("uint16", 16, "ts16", "rho")
    for b in range(8):
        s["pb%d" % b] = ("psum", [128, 512], "float32")
    return s


SCRATCH = _scratch()
SEMAPHORES = (["vec", "sca", "ten", "gps", "dx0", "dx1", "du", "dp", "dw", "dv", "dq", "dy", "dl", "loc"]
              + ["ca%d" % t for t in range(ROUNDS)] + ["la%d" % t for t in range(ROUNDS)])


def rank_program(g, core, T, topo):
    rank = T.rank_of(core)
    if rank is None:
        return
    n = len(T.cores)
    nxt, prv = T.cores[(rank + 1) % n], T.cores[(rank - 1) % n]
    mask = topo.mask(core, nxt)
    n_out, n_in = len(topo.engines(core, nxt)), len(topo.engines(prv, core))
    rid, pid = topo.addr(nxt, core)
    V, S, P, Y = g.vector, g.scalar, g.tensor, g.sync
    queue = {"v": V, "s": S, "t": P, "g": g, "y": Y}
    own_sem = {"v": "vec", "s": "sca", "t": "ten", "g": "gps"}
    count = {"vec": 0, "sca": 0, "ten": 0, "gps": 0, "loc": 0}
    waited = {}
    writer, readers = {}, {}

    def W(name, a=0, b=None, step=1):
        buf, lo, w = PLACE[name]
        return T[buf][:, lo + a:lo + (w if b is None else b):step]

    def wait(q, tok):
        sem, val = tok
        if waited.get((q, sem), 0) < val:
            queue[q].wait_ge(T.sem[sem], val)
            waited[(q, sem)] = val

    def order(q, reads, writes, chained=False):
        need = {}
        for k in reads:
            tok = writer[k]
            need[tok[0]] = max(need.get(tok[0], 0), tok[1])
        for k in writes:
            for tok in ([] if chained or k not in writer else [writer[k]]) + readers.get(k, []):
                need[tok[0]] = max(need.get(tok[0], 0), tok[1])
        for sem in need:
            wait(q, (sem, need[sem]))

    def note(tok, reads, writes):
        TRACE.append((reads, writes))
        for k in reads:
            readers.setdefault(k, []).append(tok)
        for k in writes:
            writer[k] = tok
            readers[k] = []

    def do(q, reads, writes, call, chained=False):
        order(q, reads, writes, chained)
        sem = own_sem[q]
        call().then_inc(T.sem[sem], 1)
        count[sem] += 1
        note((sem, count[sem]), reads, writes)

    def load(q, buf, out, src, sem, total):
        queue[q].dma_start(out, src).then_inc(T.sem[sem], 16)
        note((sem, total), [], [buf])

    def send(out, src, sem, reads):
        order("g", reads, [])
        g.remote_dma(out, src, T.sem[sem], T.sem.loc, pid, rid, mask)
        count["loc"] += n_out

    def tt(out, a, b, op, reads, writes):
        do("v", reads, writes, lambda: V.tensor_tensor(out, a, b, op))

    def ts(out, a, s1, op0, reads, writes, s2=None, op1=None):
        if op1 is None:
            do("v", reads, writes, lambda: V.tensor_scalar(out, a, s1, None, op0))
        else:
            do("v", reads, writes, lambda: V.tensor_scalar(out, a, s1, s2, op0, op1))

    def cp(out, a, reads, writes):
        do("v", reads, writes, lambda: V.tensor_copy(out, a))

    def act(out, a, scale, reads, writes, func=AF.Copy, bias=0.0):
        if func == AF.Copy:
            do("s", reads, writes, lambda: S.activation(out, a, func, scale=scale))
        else:
            do("s", reads, writes, lambda: S.activation(out, a, func, bias=bias, scale=scale))

    def scan(out, d0, d1, reads, writes, init=0.0, op0=OP.mult, op1=OP.add):
        do("v", reads, writes, lambda: V.tensor_tensor_scan(out, d0, d1, init, op0, op1))

    def quant(name, tile, reads, a=0, b=None, keys=None):
        b = T["q" + name].shape[1] if b is None else b
        do("v", reads, keys or ["q" + name], lambda: V.quantize_mx(T["q" + name][:, a:b], T["s" + name][:, a:b], tile[:, 4 * a:4 * b]))

    def fillc(out, value, key):
        do("v", [], key, lambda: V.memset(out, value))

    def fills(out, n, value, key):
        act(out, T.irow[:, 0:n], 0.0, ["irow"], key, AF.Identity, value)

    def iota(out, pattern, cm, key, base=0):
        do("g", [], [key], lambda: g.iota(out, pattern, base, cm, allow_small_or_imprecise_dtypes=True))

    def mm(bank, a, x, k, reads, start=True, stop=True, col=0, first=0):
        do("t", reads, ["pb%d" % bank],
           lambda: P.matmul_mx(T["pb%d" % bank][:, 0:k], T["q" + a][:, col:col + 128], T["s" + a][:, col:col + 128], T["q" + x][:, first:first + k], T["s" + x][:, first:first + k], start, stop), chained=not start)

    def five(j):
        return T.fy[:, 59 + 16 * j:1328:80]

    load("s", "usb", T.usb[:], T.u[:], "du", 16)
    load("y", "x0_0", T.x0[:, 0:512], T.x[:, 0:512], "dx0", 16)
    load("y", "lst0", T.lst0[:], T.p[:], "dp", 16)
    load("y", "x0_1", T.x0[:, 512:1024], T.x[:, 512:1024], "dx1", 16)
    load("y", "qw", T.qw[:].bitcast(dt.uint8), T.wc[:], "dw", 32)
    load("y", "qw", T.sw[:], T.ws[:], "dw", 32)
    load("y", "vsb", T.vsb[:], T.v[:], "dv", 16)
    iota(T.ipcol[:], [[1, 1]], 1, "ipcol")
    iota(T.irow[:], [[1, 512]], 0, "irow")
    iota(T.t16[:], [[0, 17], [1, 16]], 0, "t16")

    slot_keys = {name: ["c%s%d" % (name, i) for i in range(4)] for name in CTILES}
    slot_keys["a"] = ["blk0", "blk1"] + slot_keys["a"][1:]
    at = {m: 8 * m * (m - 1) for m in range(1, 16)}
    views = {}
    for name, (buf, c0, slots) in CTILES.items():
        for i, m in enumerate(slots):
            if m != "b":
                views[m] = (T["c" + buf][:, 4 * c0 + i:4 * c0 + 64 * m:4], "c%s%d" % (name, i))
    V0, VF, SF, PC = 0, 2, 3, 4
    UNPACK = [5, 6, 7, 1]
    SCORES = [(V0, 0), (VF, 128)]
    both = lambda name, b: ["%s0%d" % (name, b), "%s1%d" % (name, b)]
    four = lambda name, hf: ["%s%d%d" % (name, hf, b) for b in range(4)]
    half = lambda hf: slice(128 * hf, 128 * hf + 128)
    wide = lambda hf: slice(512 * hf, 512 * hf + 512)
    part = lambda hf, b: slice(512 * hf + b, 512 * hf + 512, 4)
    score = lambda hf: T["pb%d" % SCORES[hf][0]][:, SCORES[hf][1]:SCORES[hf][1] + 128]

    def x_keys(t, hf):
        return ["x0_%d" % hf] * 4 if t == 0 else four("x", hf)

    def zeros(name):
        buf, c0, slots = CTILES[name]
        lo = 4 * (c0 + 16 * slots[3])
        act(T["c" + buf][:, lo:lo + 192], T.ee[:, 0:192], 1.0, ["ee"], slot_keys[name][-4:])

    def row(t, m):
        bank = V0 if m <= 8 else VF
        view, key = views[m]
        ts(view, T["pb%d" % bank][:, 0:16 * m], T.ffw[:, 16 * m + 15:16 * m + 16], OP.is_lt, ["pb%d" % bank, "ffw%d" % (m // 8)], [key])

    def count_row(t, m):
        view, key = views[m]
        do("s", [key], ["junk%d" % m, "rs%d" % m], lambda: S.activation(T.junk[:, at[m]:at[m] + 16 * m], view, AF.Copy, accum_out=W("rs", m, m + 1)))

    def sign_row(t, m):
        act(T.sgn[:, at[m]:at[m] + 16 * m], T["pb%d" % SF][:, 0:16 * m], -1.0, ["pb%d" % SF, "ffw%d" % (m // 8)], ["sgn%d" % m], AF.Sign, T.ffw[:, 16 * m + 15:16 * m + 16])

    def keep_row(t, m):
        view, key = views[m]
        do("s", ["sgn%d" % m], [key, "rs%d" % m], lambda: S.activation(view, T.sgn[:, at[m]:at[m] + 16 * m], AF.Relu, accum_out=W("rs", m, m + 1)))

    def sum_a(t):
        quant("ca", T.ca, slot_keys["a"])
        mm(PC, "g", "ca", 256, ["qg", "qca"], True, False)

    def sum_b(t):
        quant("cb", T.cb, slot_keys["b"] + slot_keys["d"], 0, 256)
        mm(PC, "g", "cb", 192, ["qcb"], False, False)
        mm(PC, "g", "cb", 128, ["qcb"], False, False, first=192)

    def sum_c(t):
        quant("cc", T.cc, slot_keys["c"])
        mm(PC, "g", "cc", 128, ["qcc"], False, True)

    def quant_state(t, hf):
        x = "x%d" % t
        quant(x, T[x], x_keys(t, hf), 128 * hf, 128 * hf + 128, ["qx%d" % hf])
        if t == ROUNDS:
            mm(hf, "v", x, 128, ["qv", "qx%d" % hf], first=128 * hf)
        elif hf == 1:
            mm(VF, "r", x, 256, ["qx0", "qx1"])
            mm(SF, "r", x, 256, ["qx0", "qx1"])
            send(T["ql%d" % t][:].bitcast(dt.uint8), T["q" + x][:].bitcast(dt.uint8), "ca%d" % t, ["qx0", "qx1"])
            send(T["sl%d" % t][:], T["s" + x][:], "ca%d" % t, ["qx0", "qx1"])
            note(("ca%d" % t, 2 * n_in), [], ["ql"])
        elif t > 0:
            mm(V0, "r", x, 128, ["qr", "qrs", "qx0"])

    def pick_scales(t):
        do("s", ["qu", "u16"], ["qrs"], lambda: S.activation(T.sr[:], T.su[:].indirect(T.u16[:]), AF.Copy))
        mm(V0, "r", "x0", 128, ["qr", "qrs", "qx0"])

    def landings(t):
        ls, la = "ls%d" % (t + 1), "la%d" % t
        ts(T[ls][:], W("mo", 3, 80, 5), -WHOLE, OP.add, ["mo"], ["ls"])
        send(T[la][:], T[ls][:], la, ["ls"])
        note((la, n_in), [], ["la"])

    def packed_row(t, a=0, b=4):
        if t < ROUNDS:
            tt(W("vr", 64 * a, 64 * b), T.irow[:].indirect(T["ls%d" % t][:, 4 * a:4 * b]), W("irs", 64 * a, 64 * b), OP.subtract, ["irow", "ls", "irs"], ["vr%d" % i for i in range(a, b)])

    def store_landings(t):
        if t == ROUNDS - 1:
            act(W("lr"), T.irow[:].indirect(T["ls%d" % ROUNDS][:]), 1.0, ["irow", "ls"], ["lr"])
            order("y", ["lr"], [])
            lo = PLACE["lr"][1]
            Y.dma_start(T.ol[:], T.rows[0:128:16, lo:lo + 256]).then_inc(T.sem.dl, 16)

    def unpack(t, b):
        mm(UNPACK[b], "e", "l%d" % t, 256, ["qe%d" % b, "ql"], col=128 * b)
        act(T["h%d" % t][:, 512 * b:512 * b + 256], T["pb%d" % UNPACK[b]][:, 0:256], 0.5, ["pb%d" % UNPACK[b]], ["hd%d" % b])

    def catch(t, cols, offsets, b, keys):
        tt(T["z%d" % t][:, cols], T["h%d" % t][:, 512 * b:512 * b + 512].indirect(offsets), T.xh[:, cols], OP.add, ["ts" + k[1] for k in keys] + ["xh", "hx%d" % b, "hd%d" % b], keys)

    def layer(t, hf):
        z = "z%d" % t
        quant(z, T[z], four("z", hf), 128 * hf, 128 * hf + 128, ["qz%d" % hf])
        for b in range(4):
            mm(4 * hf + b, "w", z, 128, ["qw", "qz%d" % hf], col=128 * b, first=128 * hf)

    STEP = {
        "ee": lambda t: fillc(T.ee[:], 0.0, ["ee"]),
        "za": lambda t: zeros("a"), "zb": lambda t: zeros("b"), "zc": lambda t: zeros("c"), "zd": lambda t: zeros("d"),
        "ones": lambda t: fillc(T.d0b[:], 1.0, ["d0b"]), "onesb": lambda t: fillc(T.d0b[:, 0:256:16], 0.0, ["d0b"]),
        "flat": lambda t: fillc(T.d0r[:], 0.0, ["d0r"]), "flatb": lambda t: fillc(T.d0r[:, 0:256:16], -2 * BIG, ["d0r"]),
        "ik": lambda t: ts(T.ik[:], T.ipcol[:], 15, OP.bitwise_and, ["ipcol"], ["ik"]),
        "ig": lambda t: ts(T.ig[:], T.ipcol[:], 4, OP.arith_shift_right, ["ipcol"], ["ig"]),
        "pcol": lambda t: cp(W("pcol"), T.ipcol[:], ["ipcol"], ["pcol"]),
        "qzero": lambda t: do("v", ["ee"], ["qcb"], lambda: V.quantize_mx(T.qcb[:, 192:320], T.scb[:, 192:320], T.ee[:, 0:512])),
        "k": lambda t, m=None: cp(W("k"), T.ik[:], ["ik"], ["k"]) if m is None else keep_row(t, m),
        "ktwo": lambda t: ts(W("k2"), T.ik[:], 2.0, OP.add, ["ik"], ["k2"]),
        "mid": lambda t: ts(W("mid"), T.ig[:], -64.0, OP.mult, ["ig"], ["mid"], -31.5, OP.add),
        "last": lambda t: ts(W("e15"), T.ik[:], 15.0, OP.is_equal, ["ik"], ["e15"], LIFT, OP.mult),
        "pickl": lambda t: cp(T.u16[:], T.irow[:, 0:128:16], ["irow"], ["u16"]),
        "eye": lambda t: ts(T.ee[:, 4:516:4], T.irow[:, 0:128], W("pcol"), OP.is_equal, ["irow", "pcol"], ["ee"]),
        "irs": lambda t: act(W("irs"), T.irow[:, 0:256], 1.0 / 1024.0, ["irow"], ["irs"]),
        "gj": lambda t: act(T.gj[:], T.irow[:], 1.0, ["irow", "mid"], ["gj"], AF.Abs, W("mid")),
        "offr": lambda t: ts(W("offr"), W("e15"), W("k"), OP.subtract, ["e15", "k"], ["offr"], 15.0 - LIFT - SINK, OP.add),
        "offc": lambda t: ts(W("offc"), W("k"), W("e15"), OP.subtract, ["e15", "k"], ["offc"], LIFT + WHOLE / 1024, OP.add),
        "lzero": lambda t: cp(T.ls0[:], T.lst0[:], ["lst0"], ["ls"]),
        "cfive": lambda t: ts(five(4), T.irow[:, 0:256:16], W("offc"), OP.add, ["irow", "offc"], ["five4"], -1024.0, OP.mult),
        "kwa": lambda t: act(T.kwa[:], T.t16[:], -1.0, ["t16", "k2"], ["kwa"], AF.Relu, W("k2")),
        "kwb": lambda t: act(T.kwb[:], T.kwa[:], 7 * LIFT, ["kwa"], ["kwb"], AF.Abs, -4 * LIFT),
        "ctl": lambda t: act(T.ctl[:], T.kwb[:], -1.0, ["kwb"], ["ctl"], AF.Identity, 4 * LIFT),
        "cw": lambda t: act(T.cw[:], T.kwb[:, 0:256], -1.0, ["kwb"], ["cw"], AF.Identity, 4 * LIFT),
        "cy": lambda t: act(W("cy"), T.kwb[:, 0:256], -1024.0, ["kwb"], ["cy"], AF.Identity, 4096 * LIFT),
        "mask": lambda t: ts(T.fmsk[:], T.t16[:, 0:256], W("k"), OP.not_equal, ["t16", "k"], ["fmsk"], -BIG, OP.mult),
        "rlist": lambda t: act(W("r16"), T.irow[:, 0:256:16], 1.0, ["irow", "offr"], ["r16"], AF.Identity, W("offr")),
        "rzero": lambda t: fills(W("rs", 0, 1), 1, 0.0, ["rs0"]),
        "qu": lambda t: quant("u", T.usb, ["usb"]), "qv": lambda t: quant("v", T.vsb, ["vsb"]), "qxx": lambda t: quant_state(0, 0),
        "pick": lambda t: do("v", ["qu", "u16"], ["qr"], lambda: V.tensor_copy(T.qr[:].bitcast(dt.uint32), T.qu[:].bitcast(dt.uint32).indirect(T.u16[:]))),
        "picks": pick_scales,
        "gg": lambda t: ts(T.gg[:], T.gj[:], 32.0, OP.is_lt, ["gj"], ["gg"]),
        "qg": lambda t: quant("g", T.gg, ["gg"]),
        "qe": lambda t, b: do("v", ["ee"], ["qe%d" % b], lambda: V.quantize_mx(T.qe[:, 128 * b:128 * b + 128], T.se[:, 128 * b:128 * b + 128], T.ee[:, 4 - b:516 - b])),
        "whole": lambda t: ts(W("mo", 3, 80, 5), T.lst0[:], WHOLE, OP.add, ["lst0"], ["mo"]),
        "own": lambda t: tt(W("mo", 4, 80, 5), W("mo", 3, 80, 5), five(4), OP.add, ["mo", "five4"], ["own"]),
        "offl": lambda t: act(W("offl"), W("e15"), -1.0, ["e15"], ["offl"], AF.Identity, LIFT - WHOLE),
        "offk": lambda t: act(W("offk"), W("e15"), 1.0, ["e15"], ["offk"], AF.Identity, 256.0 - LIFT),
        "fthree": lambda t: fills(five(3), 16, WHOLE, ["five3"]),
        "mzone": lambda t: fills(W("mz"), 80, 1.0, ["mz"]),
        "mzzero": lambda t: fills(W("mz", 0, 80, 5), 16, 0.0, ["mz"]),
        "mzstep": lambda t: fills(W("mz", 1, 80, 5), 16, -1024.0, ["mz"]),
        "ibf": lambda t: act(T.ibf[:], T.irow[:, 0:256], 1.0, ["irow"], ["ibf"]),
        "ibn": lambda t: act(T.ibn[:], T.irow[:, 0:256], 1.0, ["irow"], ["ibn"], AF.Identity, -256.0),
        "wa": lambda t: fills(T.w[:, 0:512], 512, 0.0, ["w"]), "wb": lambda t: fills(T.w[:, 512:768], 256, 0.0, ["w"]),
        "qx": quant_state,
        "min": lambda t, hf: tt(T.fd1[:, half(hf)], score(hf), T.fmsk[:, half(hf)], OP.add, ["pb%d" % SCORES[hf][0], "fmsk"], ["fd%d" % hf]),
        "scan": lambda t, hf: scan(T.ffw[:, half(hf)], T.d0r[:, half(hf)], T.fd1[:, half(hf)], ["d0r", "fd%d" % hf], ["ffw%d" % hf], -BIG, OP.add, OP.max),
        "blocks": lambda t: tt(T.ca[:, 0:1024:4], T["pb%d" % VF][:, 0:256], T.ffw[:], OP.is_le, ["pb%d" % VF, "ffw0", "ffw1"], ["blk0", "blk1"]),
        "blk": lambda t, hf: tt(T.ca[:, part(hf, 0)], score(hf), T.ffw[:, half(hf)], OP.is_le, ["pb%d" % SCORES[hf][0], "ffw%d" % hf], ["blk%d" % hf]),
        "r": row, "c": count_row, "s": sign_row, "qa": sum_a, "qb": sum_b, "qc": sum_c,
        "bsum": lambda t: scan(T.bsum[:], T.d0b[:], T.ca[:, 0:1024:4], ["d0b", "blk0", "blk1"], ["bsum"]),
        "qone": lambda t: tt(W("q1"), W("r16"), T.bsum[:, 15:256:16], OP.subtract, ["r16", "bsum"], ["q1"]),
        "qtwo": lambda t: tt(T.ctl[:, 16:272:16], W("q1"), W("rs"), OP.subtract, ["q1"] + ["rs%d" % m for m in range(16)], ["ctl"]),
        "ex": lambda t: scan(W("ex"), T["pb%d" % PC][:, 0:256], T.ctl[:, 1:257], ["ctl", "pb%d" % PC], ["ex"], 0.0, OP.max, OP.add),
        "rho": lambda t: ts(T.rho[:], W("ex", 15, 256, 16), SINK, OP.add, ["ex"], ["rho"]),
        "lzer": lambda t: act(five(0), W("mo", 3, 80, 5), 1.0, ["mo", "offl"], ["five0"], AF.Identity, W("offl")),
        "ltwo": lambda t: act(five(2), W("mo", 3, 80, 5), 1.0, ["mo"], ["five2"], AF.Identity, -WHOLE),
        "put": lambda t: cp(W("pw").indirect(T.rho[:]), W("vr"), ["rho", "vr0", "vr1", "vr2", "vr3"], ["pw"]),
        "swaps": lambda t: act(W("pv", 0, 256, 2), W("pw", 1, 256, 2), 1.0, ["pw"], ["pve"]),
        "swapw": lambda t: cp(W("pv", 0, 256, 2), W("pw", 1, 256, 2), ["pw"], ["pve"]),
        "swapv": lambda t: cp(W("pv", 1, 256, 2), W("pw", 0, 256, 2), ["pw"], ["pvo"]),
        "get": lambda t: ts(W("yy"), W("pv").indirect(T.rho[:]), 1024.0, OP.mult, ["pve", "pvo", "rho"], ["yy0", "yy1"]),
        "fy": lambda t: scan(T.fy[:, 0:1280:5], W("cy"), W("yy"), ["cy", "yy0", "yy1"], ["five10", "five11"], 0.0, OP.add, OP.max),
        "ss": lambda t: tt(W("ss"), five(1), W("mo", 4, 80, 5), OP.add, ["five10", "five11", "own"], ["ss"]),
        "bits": lambda t: ts(W("tt"), W("ss"), FIELD, OP.bitwise_and, ["ss"], ["tt"]),
        "ok": lambda t: ts(W("mz", 2, 80, 5), W("tt"), 0.0, OP.is_equal, ["tt"], ["mz"], 1.0 / 1024.0, OP.mult),
        "five": lambda t: scan(W("mo"), W("mz"), T.fy[:, 59:1328:16], ["mz", "five0", "five10", "five11", "five2", "five3", "five4"], ["mo", "own"]),
        "geth": lambda t, hf: ts(W("yy", 128 * hf, 128 * hf + 128), W("pv").indirect(T.rho[:, 8 * hf:8 * hf + 8]), 1024.0, OP.mult, ["pve", "pvo", "rho"], ["yy%d" % hf]),
        "fyh": lambda t, hf: scan(T.fy[:, 640 * hf:640 * hf + 640:5], W("cy", 128 * hf, 128 * hf + 128), W("yy", 128 * hf, 128 * hf + 128), ["cy", "yy%d" % hf], ["five1%d" % hf], 0.0, OP.add, OP.max),
        "ls": landings, "ol": store_landings,
        "vr": lambda t, a=0, b=4: packed_row(t + 1, a, b),
        "mine": lambda t: cp(T.w[:, 256:768].indirect(T["ls%d" % (t + 1)][:]), T.ibf[:], ["ls", "ibf"], ["w"]),
        "theirs": lambda t: cp(T.w[:, 0:512].indirect(T["la%d" % t][:]), T.ibn[:], ["la", "ibn"], ["w"]),
        "src": lambda t: scan(T.src[:], T.cw[:], T.w[:, 256:512], ["cw", "w"], ["src0", "src1"], 0.0, OP.add, OP.max),
        "ts": lambda t: ts(T.ts16[:], T.src[:, 15:256:16], W("offk"), OP.add, ["src0", "src1", "offk"], ["ts0", "ts1"]),
        "srch": lambda t, hf: scan(T.src[:, half(hf)], T.cw[:, half(hf)], T.w[:, 256 + 128 * hf:384 + 128 * hf], ["cw", "w"], ["src%d" % hf], 0.0, OP.add, OP.max),
        "tsh": lambda t, hf: ts(T.ts16[:, 8 * hf:8 * hf + 8], T.src[:, 128 * hf + 15:128 * hf + 128:16], W("offk"), OP.add, ["src%d" % hf, "offk"], ["ts%d" % hf]),
        "hx": lambda t, b: act(T["h%d" % t][:, 512 * b + 256:512 * b + 512], T["x%d" % t][:, b:1024:4], 0.5, x_keys(t, 0) + x_keys(t, 1), ["hx%d" % b]),
        "xh": lambda t: act(T.xh[:], T["x%d" % t][:], 0.5, x_keys(t, 0) + x_keys(t, 1), ["xh"]),
        "hd": unpack,
        "G": lambda t, b: catch(t, slice(b, 1024, 4), T.ts16[:], b, both("z", b)),
        "g": lambda t, hf, b: catch(t, part(hf, b), T.ts16[:, 8 * hf:8 * hf + 8], b, ["z%d%d" % (hf, b)]),
        "Z": lambda t, b: act(T.zz[:, b:1024:4], T["z%d" % t][:, b:1024:4], 32.0, both("z", b), both("zz", b)),
        "z": lambda t, hf, b: act(T.zz[:, part(hf, b)], T["z%d" % t][:, part(hf, b)], 32.0, ["z%d%d" % (hf, b)], ["zz%d%d" % (hf, b)]),
        "qz": layer,
        "a": lambda t, hf, b: tt(T.ab[:, part(hf, b)], T["pb%d" % (4 * hf + b)][:, 0:128], T.zz[:, part(hf, b)], OP.add, ["pb%d" % (4 * hf + b), "zz%d%d" % (hf, b)], ["ab%d%d" % (hf, b)]),
        "xv": lambda t, hf: ts(T["x%d" % (t + 1)][:, wide(hf)], T.ab[:, wide(hf)], 0.03125, OP.mult, four("ab", hf), four("x", hf)),
        "xs": lambda t, hf: act(T["x%d" % (t + 1)][:, wide(hf)], T.ab[:, wide(hf)], 0.03125, four("ab", hf), four("x", hf)),
        "xb": lambda t, hf, b: act(T["x%d" % (t + 1)][:, part(hf, b)], T.ab[:, part(hf, b)], 0.03125, ["ab%d%d" % (hf, b)], ["x%d%d" % (hf, b)]),
    }
    STATE = ("a", "xv", "xs", "xb", "z", "Z", "g", "qz", "vr")

    def step(word, t):
        name = word.rstrip("0123456789")
        digits = word[len(name):]
        TRACE.append(word)
        STEP[name](t, *([int(digits)] if digits and name in "rcsk" else [int(d) for d in digits]))

    for word in START.split():
        step(word, -1)
    words = ROUND.split()
    front = words.index("ls")
    for t in range(ROUNDS + 1):
        for i, word in enumerate(words):
            name = word.rstrip("0123456789*")
            if word.endswith("*") and t > 0:
                continue
            if name in STATE or word == "qx0":
                late = i < front
                if late and t > 0 or not late and t < ROUNDS:
                    step(word, t - late + (word == "qx0"))
            elif t < ROUNDS or word == "qx1":
                step(word.rstrip("*"), t)

    q = "x%d" % ROUNDS
    act(T.ysb[:, 0:128], T.pb0[:, 0:128], 1.0, ["pb0"], ["ysb0"])
    order("s", ["ysb0"], [])
    S.dma_start(T.y[:, 0:128], T.ysb[:, 0:128]).then_inc(T.sem.dy, 16)
    order("y", ["qx0", "qx1"], [])
    Y.dma_start(T.oc[:], T["q" + q][:].bitcast(dt.uint8)).then_inc(T.sem.dq, 16)
    for k in range(4):
        Y.dma_start(T.osc[4 * k:4 * k + 4, :], T["s" + q][32 * k:32 * k + 4, :]).then_inc(T.sem.dq, 16)
    act(T.ysb[:, 128:256], T.pb1[:, 0:128], 1.0, ["pb1"], ["ysb1"])
    order("s", ["ysb1"], [])
    S.dma_start(T.y[:, 128:256], T.ysb[:, 128:256]).then_inc(T.sem.dy, 16)
    for sem in ("vec", "sca", "ten", "gps", "loc"):
        wait("g", (sem, count[sem]))
    for sem, val in (("dx0", 16), ("dx1", 16), ("du", 16), ("dp", 16), ("dw", 32), ("dv", 16), ("dq", 80), ("dy", 32), ("dl", 16)):
        wait("g", (sem, val))
    for t in range(ROUNDS):
        wait("g", ("ca%d" % t, 2 * n_in))
        wait("g", ("la%d" % t, n_in))
